import numpy as np
import ml_dtypes


def mxq(x, axis, fmt="e4m3"):
    dtype, down = {"e4m3": (ml_dtypes.float8_e4m3fn, 7), "e5m2": (ml_dtypes.float8_e5m2, 14)}[fmt]
    v = np.moveaxis(np.asarray(x, np.float32).astype(ml_dtypes.bfloat16).astype(np.float64), axis, -1)
    blocks = v.reshape(v.shape[:-1] + (-1, 32))
    amax = np.abs(blocks).max(-1, keepdims=True)
    byte = np.maximum(np.where(amax > 0, np.frexp(amax)[1] - 1 + 127, 0) - down, 1)
    scale = np.exp2(byte - 127.0)
    codes = (blocks / scale).astype(np.float32).astype(dtype).astype(np.float64)
    return np.moveaxis((codes * scale).reshape(v.shape), -1, axis)


WIDE = False


def mx_kscale(k):
    if not WIDE:
        return np.ones(k)
    levels = np.array([18, -18])
    if k % 512:
        return np.exp2(np.random.permutation(np.resize(levels, k // 32))).repeat(32)
    a = np.empty((k // 512, 16))
    for p in range(k // 512):
        a[p, :8] = np.random.permutation(np.resize(levels, 8))
        for g in range(8):
            far = levels[np.abs(levels - a[p, g]) >= 10]
            a[p, g + 8] = far[np.random.randint(len(far))]
    return np.exp2(a.ravel()).repeat(32)


def f64(x):
    return np.asarray(x).astype(np.float64)


def striped(idx):
    return np.tile(np.asarray(idx).reshape(-1, 16).T, (8, 1)).astype(np.uint16)


def unstriped(offs):
    return offs[:16].T.reshape(-1).astype(np.int64)


def setup_inputs():
    n = np.random.standard_normal
    uni = np.random.uniform
    src = np.random.randint(0, 512, 1024)
    dst = np.random.randint(0, 512, 1024)
    f_m = mx_kscale(512)
    return {
        "W": (n((512, 512)) / np.sqrt(512) * f_m[:, None]).astype(np.float32),
        "dyT": (n((512, 512)) / f_m[:, None]).astype(np.float32),
        "xT": (n((512, 512))).astype(np.float32),
        "soffs": striped(src),
        "toffs": striped(dst),
    }


def reference(W, dyT, xT, soffs, toffs):
    src = unstriped(soffs)
    dst = unstriped(toffs)
    u = mxq(f64(W), 0, "e4m3").T @ mxq(f64(dyT), 0, "e5m2")
    xs = f64(xT)[:, src]
    ud = u[:, dst]
    out = xs * ud
    return out

@@ -1,0 +1,123 @@
+from contextlib import ExitStack
+
+import concourse.mybir as mybir
+
+M, D, X, C = 512, 512, 512, 1024
+FLOPS = 2 * M * D * X
+
+F32 = mybir.dt.float32
+BF16 = mybir.dt.bfloat16
+U32 = mybir.dt.uint32
+U16 = mybir.dt.uint16
+U8 = mybir.dt.uint8
+E4M3X4 = mybir.dt.float8_e4m3fn_x4
+E5M2X4 = mybir.dt.float8_e5m2_x4
+MULT = mybir.AluOpType.mult
+
+P = 128
+PACK = 4
+LANES = 16
+BLOCKS = D // P
+WINDOW = X + LANES
+HALF = D // 2
+PIECE = 512
+LAST_PIECES = (512, 256, 128, 128)
+
+
+def interleave(nc, grouped, raw):
+    nc.scalar.copy(
+        grouped[:].rearrange("p (c i) t -> p c t i", i=4),
+        raw[:].rearrange("p t (c i) -> p c t i", i=4),
+    )
+
+
+def tile_attend_gcfconv_f_kernel(tc, W, dyT, xT, soffs, toffs, out):
+    nc = tc.nc
+    with ExitStack() as ctx:
+        keep = ctx.enter_context(tc.tile_pool(name="keep", bufs=1))
+        psum = ctx.enter_context(tc.psum_pool(name="psum", bufs=1))
+
+        src = keep.tile([P, C // LANES], U16, name="src")
+        dst = keep.tile([P, C // LANES], U16, name="dst")
+        x_win = [keep.tile([P, WINDOW], F32, name=f"x_win{b}") for b in range(BLOCKS)]
+        u_win = [keep.tile([P, WINDOW], F32, name=f"u_win{b}") for b in range(BLOCKS)]
+        dy_raw = keep.tile([P, PACK, X], F32, name="dy_raw")
+        w_raw = [keep.tile([P, PACK, HALF], F32, name=f"w_raw{h}") for h in range(2)]
+        w_rows = W.rearrange("(p t) d -> p t d", t=PACK)
+
+        for win in x_win + u_win:
+            nc.gpsimd.memset(win[:, X:WINDOW], 0.0)
+
+        def load_x(b):
+            nc.sync.dma_start(x_win[b][:, 0:X], xT[b * P : (b + 1) * P, :])
+
+        def load_w(h):
+            nc.sync.dma_start(w_raw[h][:], w_rows[:, :, h * HALF : (h + 1) * HALF])
+
+        nc.sync.dma_start(src[:], soffs)
+        load_x(0)
+        load_x(1)
+        nc.sync.dma_start(dy_raw[:], dyT.rearrange("(p t) x -> p t x", t=PACK))
+        load_x(2)
+        load_w(0)
+        load_x(3)
+        load_w(1)
+        nc.sync.dma_start(dst[:], toffs)
+
+        def offsets(lst, c0, n):
+            return lst[:, c0 // LANES : (c0 + n) // LANES]
+
+        xs = [None] * BLOCKS
+
+        def gather_x(b, tag):
+            xs[b] = keep.tile([P, C], F32, name=f"xs{b}", tag=tag)
+            for c0 in range(0, C, PIECE):
+                nc.vector.tensor_copy(xs[b][:, c0 : c0 + PIECE], x_win[b][:].indirect(offsets(src, c0, PIECE)))
+
+        def quantise(raw, width, fmt, name):
+            grouped = keep.tile([P, width, PACK], BF16, name=name + "_grouped", align_bytes=64)
+            codes = keep.tile([P, width], U32, name=name + "_codes", align_bytes=64)
+            scales = keep.tile([P, width], U8, name=name + "_scales", align_bytes=64)
+            interleave(nc, grouped, raw)
+            nc.vector.quantize_mx(
+                out=codes[:].bitcast(fmt), scales=scales[:], in_=grouped[:].rearrange("p w t -> p (w t)")
+            )
+            return codes, scales
+
+        def product(b, w_codes, w_scales):
+            cols = slice((b % 2) * P, (b % 2 + 1) * P)
+            bank = psum.tile([P, X], F32, name=f"bank{b}")
+            nc.tensor.matmul_mx(
+                out=bank[:],
+                lhsT=w_codes[:, cols].bitcast(E4M3X4),
+                lhsT_scale=w_scales[:, cols],
+                rhs=dy_codes[:].bitcast(E5M2X4),
+                rhs_scale=dy_scales[:],
+                start=True,
+                stop=True,
+            )
+            nc.scalar.copy(u_win[b][:, 0:X], bank[:])
+
+        def finish(b, pieces):
+            c0 = 0
+            for n in pieces:
+                res = keep.tile([P, n], F32, name=f"res{b}_{c0}")
+                nc.vector.tensor_tensor(
+                    res[:], u_win[b][:].indirect(offsets(dst, c0, n)), xs[b][:, c0 : c0 + n], MULT
+                )
+                nc.sync.dma_start(out[b * P : (b + 1) * P, c0 : c0 + n], res[:])
+                c0 = c0 + n
+
+        for b in range(BLOCKS - 1):
+            gather_x(b, f"xs{b}")
+        dy_codes, dy_scales = quantise(dy_raw, X, E5M2X4, "dy")
+        w_q = quantise(w_raw[0], HALF, E4M3X4, "w0")
+        gather_x(BLOCKS - 1, "w_raw0")
+        product(0, *w_q)
+        product(1, *w_q)
+        w_q = quantise(w_raw[1], HALF, E4M3X4, "w1")
+        product(2, *w_q)
+        product(3, *w_q)
+        for b in range(BLOCKS - 1):
+            finish(b, (PIECE, PIECE))
+        finish(BLOCKS - 1, LAST_PIECES)

@@ -18,10 +18,11 @@ P = 128
 PACK = 4
 LANES = 16
 BLOCKS = D // P
-WINDOW = X + LANES
+X_WINDOW = 1376
+U_WINDOW = C + LANES
 HALF = D // 2
-PIECE = 512
-LAST_PIECES = (512, 256, 128, 128)
+LAST_PIECES = (640, 256, 128)
+LAST_WINDOW = max(LAST_PIECES) + LANES
 
 
 def interleave(nc, grouped, raw):
@@ -39,23 +40,28 @@ def tile_attend_gcfconv_f_kernel(tc, W, dyT, xT, soffs, toffs, out):
 
         src = keep.tile([P, C // LANES], U16, name="src")
         dst = keep.tile([P, C // LANES], U16, name="dst")
-        x_win = [keep.tile([P, WINDOW], F32, name=f"x_win{b}") for b in range(BLOCKS)]
-        u_win = [keep.tile([P, WINDOW], F32, name=f"u_win{b}") for b in range(BLOCKS)]
+        x_all = keep.tile([P, (BLOCKS - 1) * X + X_WINDOW], F32, name="x_all")
+        u_widths = [U_WINDOW] * (BLOCKS - 1) + [LAST_WINDOW]
+        u_win = [keep.tile([P, u_widths[b]], F32, name=f"u_win{b}") for b in range(BLOCKS)]
         dy_raw = keep.tile([P, PACK, X], F32, name="dy_raw")
         w_raw = [keep.tile([P, PACK, HALF], F32, name=f"w_raw{h}") for h in range(2)]
         w_rows = W.rearrange("(p t) d -> p t d", t=PACK)
 
-        for win in x_win + u_win:
-            nc.gpsimd.memset(win[:, X:WINDOW], 0.0)
+        nc.vector.memset(x_all[:, BLOCKS * X :], 0.0)
+        for win in u_win:
+            nc.gpsimd.memset(win[:, X:], 0.0)
+
+        def x_start(b):
+            return (BLOCKS - 1 - b) * X
 
         def load_x(b):
-            nc.sync.dma_start(x_win[b][:, 0:X], xT[b * P : (b + 1) * P, :])
+            nc.sync.dma_start(x_all[:, x_start(b) : x_start(b) + X], xT[b * P : (b + 1) * P, :])
 
         def load_w(h):
             nc.sync.dma_start(w_raw[h][:], w_rows[:, :, h * HALF : (h + 1) * HALF])
 
-        nc.sync.dma_start(src[:], soffs)
         load_x(0)
+        nc.sync.dma_start(src[:], soffs)
         load_x(1)
         nc.sync.dma_start(dy_raw[:], dyT.rearrange("(p t) x -> p t x", t=PACK))
         load_x(2)
@@ -71,8 +77,7 @@ def tile_attend_gcfconv_f_kernel(tc, W, dyT, xT, soffs, toffs, out):
 
         def gather_x(b, tag):
             xs[b] = keep.tile([P, C], F32, name=f"xs{b}", tag=tag)
-            for c0 in range(0, C, PIECE):
-                nc.vector.tensor_copy(xs[b][:, c0 : c0 + PIECE], x_win[b][:].indirect(offsets(src, c0, PIECE)))
+            nc.vector.tensor_copy(xs[b][:], x_all[:, x_start(b) : x_start(b) + X_WINDOW].indirect(src[:]))
 
         def quantise(raw, width, fmt, name):
             grouped = keep.tile([P, width, PACK], BF16, name=name + "_grouped", align_bytes=64)
@@ -119,5 +124,5 @@ def tile_attend_gcfconv_f_kernel(tc, W, dyT, xT, soffs, toffs, out):
         product(2, *w_q)
         product(3, *w_q)
         for b in range(BLOCKS - 1):
-            finish(b, (PIECE, PIECE))
+            finish(b, (C,))
         finish(BLOCKS - 1, LAST_PIECES)

@@ -7,6 +7,7 @@ FLOPS = 2 * M * D * X
 
 F32 = mybir.dt.float32
 BF16 = mybir.dt.bfloat16
+I32 = mybir.dt.int32
 U32 = mybir.dt.uint32
 U16 = mybir.dt.uint16
 U8 = mybir.dt.uint8
@@ -27,7 +28,7 @@ LAST_WINDOW = max(LAST_PIECES) + LANES
 
 def interleave(nc, grouped, raw):
     nc.scalar.copy(
-        grouped[:].rearrange("p (c i) t -> p c t i", i=4),
+        grouped.rearrange("p (c i) t -> p c t i", i=4),
         raw[:].rearrange("p t (c i) -> p c t i", i=4),
     )
 
@@ -43,13 +44,14 @@ def tile_attend_gcfconv_f_kernel(tc, W, dyT, xT, soffs, toffs, out):
         x_all = keep.tile([P, (BLOCKS - 1) * X + X_WINDOW], F32, name="x_all")
         u_widths = [U_WINDOW] * (BLOCKS - 1) + [LAST_WINDOW]
         u_win = [keep.tile([P, u_widths[b]], F32, name=f"u_win{b}") for b in range(BLOCKS)]
-        dy_raw = keep.tile([P, PACK, X], F32, name="dy_raw")
+        dy_raw = [keep.tile([P, PACK, HALF], F32, name=f"dy_raw{h}") for h in range(2)]
+        dy_rows = dyT.rearrange("(p t) x -> p t x", t=PACK)
         w_raw = [keep.tile([P, PACK, HALF], F32, name=f"w_raw{h}") for h in range(2)]
         w_rows = W.rearrange("(p t) d -> p t d", t=PACK)
 
-        nc.vector.memset(x_all[:, BLOCKS * X :], 0.0)
+        nc.vector.memset(x_all[:, BLOCKS * X :].bitcast(I32), 0)
         for win in u_win:
-            nc.gpsimd.memset(win[:, X:], 0.0)
+            nc.vector.memset(win[:, X:].bitcast(I32), 0)
 
         def x_start(b):
             return (BLOCKS - 1 - b) * X
@@ -57,17 +59,21 @@ def tile_attend_gcfconv_f_kernel(tc, W, dyT, xT, soffs, toffs, out):
         def load_x(b):
             nc.sync.dma_start(x_all[:, x_start(b) : x_start(b) + X], xT[b * P : (b + 1) * P, :])
 
+        def load_dy(h):
+            nc.sync.dma_start(dy_raw[h][:], dy_rows[:, :, h * HALF : (h + 1) * HALF])
+
         def load_w(h):
             nc.sync.dma_start(w_raw[h][:], w_rows[:, :, h * HALF : (h + 1) * HALF])
 
         load_x(0)
         nc.sync.dma_start(src[:], soffs)
+        load_dy(0)
         load_x(1)
-        nc.sync.dma_start(dy_raw[:], dyT.rearrange("(p t) x -> p t x", t=PACK))
+        load_dy(1)
         load_x(2)
         load_w(0)
-        load_x(3)
         load_w(1)
+        load_x(3)
         nc.sync.dma_start(dst[:], toffs)
 
         def offsets(lst, c0, n):
@@ -79,11 +85,13 @@ def tile_attend_gcfconv_f_kernel(tc, W, dyT, xT, soffs, toffs, out):
             xs[b] = keep.tile([P, C], F32, name=f"xs{b}", tag=tag)
             nc.vector.tensor_copy(xs[b][:], x_all[:, x_start(b) : x_start(b) + X_WINDOW].indirect(src[:]))
 
-        def quantise(raw, width, fmt, name):
+        def quantise(raws, fmt, name):
+            width = HALF * len(raws)
             grouped = keep.tile([P, width, PACK], BF16, name=name + "_grouped", align_bytes=64)
             codes = keep.tile([P, width], U32, name=name + "_codes", align_bytes=64)
             scales = keep.tile([P, width], U8, name=name + "_scales", align_bytes=64)
-            interleave(nc, grouped, raw)
+            for h, raw in enumerate(raws):
+                interleave(nc, grouped[:, h * HALF : (h + 1) * HALF, :], raw)
             nc.vector.quantize_mx(
                 out=codes[:].bitcast(fmt), scales=scales[:], in_=grouped[:].rearrange("p w t -> p (w t)")
             )
@@ -115,12 +123,12 @@ def tile_attend_gcfconv_f_kernel(tc, W, dyT, xT, soffs, toffs, out):
 
         for b in range(BLOCKS - 1):
             gather_x(b, f"xs{b}")
-        dy_codes, dy_scales = quantise(dy_raw, X, E5M2X4, "dy")
-        w_q = quantise(w_raw[0], HALF, E4M3X4, "w0")
+        dy_codes, dy_scales = quantise(dy_raw, E5M2X4, "dy")
+        w_q = quantise(w_raw[0:1], E4M3X4, "w0")
         gather_x(BLOCKS - 1, "w_raw0")
         product(0, *w_q)
         product(1, *w_q)
-        w_q = quantise(w_raw[1], HALF, E4M3X4, "w1")
+        w_q = quantise(w_raw[1:2], E4M3X4, "w1")
         product(2, *w_q)
         product(3, *w_q)
         for b in range(BLOCKS - 1):

@@ -13,24 +13,17 @@ U16 = mybir.dt.uint16
 U8 = mybir.dt.uint8
 E4M3X4 = mybir.dt.float8_e4m3fn_x4
 E5M2X4 = mybir.dt.float8_e5m2_x4
-MULT = mybir.AluOpType.mult
 
 P = 128
 PACK = 4
-LANES = 16
+ENTRIES_PER_COLUMN = 16
 BLOCKS = D // P
+HALF = 256
+RUN = 4
+
 X_WINDOW = 1376
-U_WINDOW = C + LANES
-HALF = D // 2
-LAST_PIECES = (640, 256, 128)
-LAST_WINDOW = max(LAST_PIECES) + LANES
-
-
-def interleave(nc, grouped, raw):
-    nc.scalar.copy(
-        grouped.rearrange("p (c i) t -> p c t i", i=4),
-        raw[:].rearrange("p t (c i) -> p c t i", i=4),
-    )
+LAST_PIECES = (576, 288, 160)
+PIECES = [(C,)] * (BLOCKS - 1) + [LAST_PIECES]
 
 
 def tile_attend_gcfconv_f_kernel(tc, W, dyT, xT, soffs, toffs, out):
@@ -39,11 +32,13 @@ def tile_attend_gcfconv_f_kernel(tc, W, dyT, xT, soffs, toffs, out):
         keep = ctx.enter_context(tc.tile_pool(name="keep", bufs=1))
         psum = ctx.enter_context(tc.psum_pool(name="psum", bufs=1))
 
-        src = keep.tile([P, C // LANES], U16, name="src")
-        dst = keep.tile([P, C // LANES], U16, name="dst")
+        src = keep.tile([P, C // ENTRIES_PER_COLUMN], U16, name="src")
+        dst = keep.tile([P, C // ENTRIES_PER_COLUMN], U16, name="dst")
+
         x_all = keep.tile([P, (BLOCKS - 1) * X + X_WINDOW], F32, name="x_all")
-        u_widths = [U_WINDOW] * (BLOCKS - 1) + [LAST_WINDOW]
-        u_win = [keep.tile([P, u_widths[b]], F32, name=f"u_win{b}") for b in range(BLOCKS)]
+        u_win = [
+            keep.tile([P, max(PIECES[b]) + ENTRIES_PER_COLUMN], F32, name=f"u_win{b}") for b in range(BLOCKS)
+        ]
         dy_raw = [keep.tile([P, PACK, HALF], F32, name=f"dy_raw{h}") for h in range(2)]
         dy_rows = dyT.rearrange("(p t) x -> p t x", t=PACK)
         w_raw = [keep.tile([P, PACK, HALF], F32, name=f"w_raw{h}") for h in range(2)]
@@ -59,31 +54,24 @@ def tile_attend_gcfconv_f_kernel(tc, W, dyT, xT, soffs, toffs, out):
         def load_x(b):
             nc.sync.dma_start(x_all[:, x_start(b) : x_start(b) + X], xT[b * P : (b + 1) * P, :])
 
-        def load_dy(h):
-            nc.sync.dma_start(dy_raw[h][:], dy_rows[:, :, h * HALF : (h + 1) * HALF])
-
-        def load_w(h):
-            nc.sync.dma_start(w_raw[h][:], w_rows[:, :, h * HALF : (h + 1) * HALF])
+        def load_half(raw, rows, h):
+            nc.sync.dma_start(raw[h][:], rows[:, :, h * HALF : (h + 1) * HALF])
 
         load_x(0)
         nc.sync.dma_start(src[:], soffs)
-        load_dy(0)
+        load_half(dy_raw, dy_rows, 0)
         load_x(1)
-        load_dy(1)
+        load_half(dy_raw, dy_rows, 1)
         load_x(2)
-        load_w(0)
-        load_w(1)
+        load_half(w_raw, w_rows, 0)
+        load_half(w_raw, w_rows, 1)
         load_x(3)
         nc.sync.dma_start(dst[:], toffs)
 
-        def offsets(lst, c0, n):
-            return lst[:, c0 // LANES : (c0 + n) // LANES]
-
-        xs = [None] * BLOCKS
-
         def gather_x(b, tag):
-            xs[b] = keep.tile([P, C], F32, name=f"xs{b}", tag=tag)
-            nc.vector.tensor_copy(xs[b][:], x_all[:, x_start(b) : x_start(b) + X_WINDOW].indirect(src[:]))
+            xs = keep.tile([P, C], F32, name=f"xs{b}", tag=tag)
+            nc.vector.tensor_copy(xs[:], x_all[:, x_start(b) : x_start(b) + X_WINDOW].indirect(src[:]))
+            return xs
 
         def quantise(raws, fmt, name):
             width = HALF * len(raws)
@@ -91,46 +79,47 @@ def tile_attend_gcfconv_f_kernel(tc, W, dyT, xT, soffs, toffs, out):
             codes = keep.tile([P, width], U32, name=name + "_codes", align_bytes=64)
             scales = keep.tile([P, width], U8, name=name + "_scales", align_bytes=64)
             for h, raw in enumerate(raws):
-                interleave(nc, grouped[:, h * HALF : (h + 1) * HALF, :], raw)
+                nc.scalar.copy(
+                    grouped[:, h * HALF : (h + 1) * HALF, :].rearrange("p (c i) t -> p c t i", i=RUN),
+                    raw[:].rearrange("p t (c i) -> p c t i", i=RUN),
+                )
             nc.vector.quantize_mx(
-                out=codes[:].bitcast(fmt), scales=scales[:], in_=grouped[:].rearrange("p w t -> p (w t)")
+                out=codes[:].bitcast(fmt), scales=scales[:], in_=grouped[:].rearrange("p c t -> p (c t)")
             )
             return codes, scales
 
-        def product(b, w_codes, w_scales):
-            cols = slice((b % 2) * P, (b % 2 + 1) * P)
-            bank = psum.tile([P, X], F32, name=f"bank{b}")
-            nc.tensor.matmul_mx(
-                out=bank[:],
-                lhsT=w_codes[:, cols].bitcast(E4M3X4),
-                lhsT_scale=w_scales[:, cols],
-                rhs=dy_codes[:].bitcast(E5M2X4),
-                rhs_scale=dy_scales[:],
-                start=True,
-                stop=True,
-            )
-            nc.scalar.copy(u_win[b][:, 0:X], bank[:])
+        def products(h, w_codes, w_scales):
+            for j in range(HALF // P):
+                b = h * (HALF // P) + j
+                cols = slice(j * P, (j + 1) * P)
+                bank = psum.tile([P, X], F32, name=f"bank{b}")
+                nc.tensor.matmul_mx(
+                    out=bank[:],
+                    lhsT=w_codes[:, cols].bitcast(E4M3X4),
+                    lhsT_scale=w_scales[:, cols],
+                    rhs=dy_codes[:].bitcast(E5M2X4),
+                    rhs_scale=dy_scales[:],
+                    start=True,
+                    stop=True,
+                )
+                nc.scalar.copy(u_win[b][:, 0:X], bank[:])
 
-        def finish(b, pieces):
+        def finish(b):
             c0 = 0
-            for n in pieces:
+            for n in PIECES[b]:
+                entries = dst[:, c0 // ENTRIES_PER_COLUMN : (c0 + n) // ENTRIES_PER_COLUMN]
                 res = keep.tile([P, n], F32, name=f"res{b}_{c0}")
                 nc.vector.tensor_tensor(
-                    res[:], u_win[b][:].indirect(offsets(dst, c0, n)), xs[b][:, c0 : c0 + n], MULT
+                    res[:], u_win[b][:].indirect(entries), xs[b][:, c0 : c0 + n], mybir.AluOpType.mult
                 )
                 nc.sync.dma_start(out[b * P : (b + 1) * P, c0 : c0 + n], res[:])
                 c0 = c0 + n
 
-        for b in range(BLOCKS - 1):
-            gather_x(b, f"xs{b}")
+        xs = [gather_x(b, f"xs{b}") for b in range(BLOCKS - 1)]
         dy_codes, dy_scales = quantise(dy_raw, E5M2X4, "dy")
-        w_q = quantise(w_raw[0:1], E4M3X4, "w0")
-        gather_x(BLOCKS - 1, "w_raw0")
-        product(0, *w_q)
-        product(1, *w_q)
-        w_q = quantise(w_raw[1:2], E4M3X4, "w1")
-        product(2, *w_q)
-        product(3, *w_q)
-        for b in range(BLOCKS - 1):
-            finish(b, (C,))
-        finish(BLOCKS - 1, LAST_PIECES)
+        w_first = quantise(w_raw[0:1], E4M3X4, "w0")
+        xs.append(gather_x(BLOCKS - 1, "w_raw0"))
+        products(0, *w_first)
+        products(1, *quantise(w_raw[1:2], E4M3X4, "w1"))
+        for b in range(BLOCKS):
+            finish(b)

@@ -7,7 +7,6 @@ FLOPS = 2 * M * D * X
 
 F32 = mybir.dt.float32
 BF16 = mybir.dt.bfloat16
-I32 = mybir.dt.int32
 U32 = mybir.dt.uint32
 U16 = mybir.dt.uint16
 U8 = mybir.dt.uint8
@@ -35,7 +34,7 @@ def tile_attend_gcfconv_f_kernel(tc, W, dyT, xT, soffs, toffs, out):
         src = keep.tile([P, C // ENTRIES_PER_COLUMN], U16, name="src")
         dst = keep.tile([P, C // ENTRIES_PER_COLUMN], U16, name="dst")
 
-        x_all = keep.tile([P, (BLOCKS - 1) * X + X_WINDOW], F32, name="x_all")
+        x_win = [keep.tile([P, X_WINDOW], F32, name=f"x_win{b}") for b in range(BLOCKS)]
         u_win = [
             keep.tile([P, max(PIECES[b]) + ENTRIES_PER_COLUMN], F32, name=f"u_win{b}") for b in range(BLOCKS)
         ]
@@ -44,15 +43,8 @@ def tile_attend_gcfconv_f_kernel(tc, W, dyT, xT, soffs, toffs, out):
         w_raw = [keep.tile([P, PACK, HALF], F32, name=f"w_raw{h}") for h in range(2)]
         w_rows = W.rearrange("(p t) d -> p t d", t=PACK)
 
-        nc.vector.memset(x_all[:, BLOCKS * X :].bitcast(I32), 0)
-        for win in u_win:
-            nc.vector.memset(win[:, X:].bitcast(I32), 0)
-
-        def x_start(b):
-            return (BLOCKS - 1 - b) * X
-
         def load_x(b):
-            nc.sync.dma_start(x_all[:, x_start(b) : x_start(b) + X], xT[b * P : (b + 1) * P, :])
+            nc.sync.dma_start(x_win[b][:, 0:X], xT[b * P : (b + 1) * P, :])
 
         def load_half(raw, rows, h):
             nc.sync.dma_start(raw[h][:], rows[:, :, h * HALF : (h + 1) * HALF])
@@ -64,13 +56,13 @@ def tile_attend_gcfconv_f_kernel(tc, W, dyT, xT, soffs, toffs, out):
         load_half(dy_raw, dy_rows, 1)
         load_x(2)
         load_half(w_raw, w_rows, 0)
-        load_half(w_raw, w_rows, 1)
         load_x(3)
+        load_half(w_raw, w_rows, 1)
         nc.sync.dma_start(dst[:], toffs)
 
         def gather_x(b, tag):
             xs = keep.tile([P, C], F32, name=f"xs{b}", tag=tag)
-            nc.vector.tensor_copy(xs[:], x_all[:, x_start(b) : x_start(b) + X_WINDOW].indirect(src[:]))
+            nc.vector.tensor_copy(xs[:], x_win[b][:].indirect(src[:]))
             return xs
 
         def quantise(raws, fmt, name):

@@ -51,10 +51,10 @@ def tile_attend_gcfconv_f_kernel(tc, W, dyT, xT, soffs, toffs, out):
 
         load_x(0)
         nc.sync.dma_start(src[:], soffs)
-        load_half(dy_raw, dy_rows, 0)
         load_x(1)
-        load_half(dy_raw, dy_rows, 1)
+        load_half(dy_raw, dy_rows, 0)
         load_x(2)
+        load_half(dy_raw, dy_rows, 1)
         load_half(w_raw, w_rows, 0)
         load_x(3)
         load_half(w_raw, w_rows, 1)

@@ -34,13 +34,15 @@ def tile_attend_gcfconv_f_kernel(tc, W, dyT, xT, soffs, toffs, out):
         src = keep.tile([P, C // ENTRIES_PER_COLUMN], U16, name="src")
         dst = keep.tile([P, C // ENTRIES_PER_COLUMN], U16, name="dst")
 
-        x_win = [keep.tile([P, X_WINDOW], F32, name=f"x_win{b}") for b in range(BLOCKS)]
-        u_win = [
-            keep.tile([P, max(PIECES[b]) + ENTRIES_PER_COLUMN], F32, name=f"u_win{b}") for b in range(BLOCKS)
-        ]
+        x_first = keep.tile([P, X_WINDOW], F32, name="x_first")
+        x_pair = keep.tile([P, X + X_WINDOW], F32, name="x_pair")
+        x_last = keep.tile([P, X_WINDOW], F32, name="x_last")
+        x_win = [x_first[:], x_pair[:, 0:X_WINDOW], x_pair[:, X:], x_last[:]]
         dy_raw = [keep.tile([P, PACK, HALF], F32, name=f"dy_raw{h}") for h in range(2)]
         dy_rows = dyT.rearrange("(p t) x -> p t x", t=PACK)
-        w_raw = [keep.tile([P, PACK, HALF], F32, name=f"w_raw{h}") for h in range(2)]
+        w_head = keep.tile([P, PACK, P], F32, name="w_head")
+        w_mid = keep.tile([P, PACK, HALF], F32, name="w_mid")
+        w_tail = keep.tile([P, PACK, P], F32, name="w_tail")
         w_rows = W.rearrange("(p t) d -> p t d", t=PACK)
 
         def load_x(b):
@@ -51,50 +53,62 @@ def tile_attend_gcfconv_f_kernel(tc, W, dyT, xT, soffs, toffs, out):
 
         load_x(0)
         nc.sync.dma_start(src[:], soffs)
-        load_x(1)
+        nc.sync.dma_start(
+            x_pair[:, 0 : 2 * X].rearrange("p (b x) -> p b x", b=2),
+            xT[P : 3 * P, :].rearrange("(b p) x -> p b x", b=2),
+        )
         load_half(dy_raw, dy_rows, 0)
-        load_x(2)
         load_half(dy_raw, dy_rows, 1)
-        load_half(w_raw, w_rows, 0)
+        nc.sync.dma_start(w_head[:], w_rows[:, :, 0:P])
         load_x(3)
-        load_half(w_raw, w_rows, 1)
+        nc.sync.dma_start(w_mid[:], w_rows[:, :, P : P + HALF])
+        nc.sync.dma_start(w_tail[:], w_rows[:, :, P + HALF : D])
         nc.sync.dma_start(dst[:], toffs)
 
         def gather_x(b, tag):
             xs = keep.tile([P, C], F32, name=f"xs{b}", tag=tag)
-            nc.vector.tensor_copy(xs[:], x_win[b][:].indirect(src[:]))
+            nc.vector.tensor_copy(xs[:], x_win[b].indirect(src[:]))
             return xs
 
-        def quantise(raws, fmt, name):
-            width = HALF * len(raws)
+        def cast(raws, name):
+            width = sum(raw[:].shape[2] for raw in raws)
             grouped = keep.tile([P, width, PACK], BF16, name=name + "_grouped", align_bytes=64)
-            codes = keep.tile([P, width], U32, name=name + "_codes", align_bytes=64)
-            scales = keep.tile([P, width], U8, name=name + "_scales", align_bytes=64)
-            for h, raw in enumerate(raws):
+            c0 = 0
+            for raw in raws:
+                n = raw[:].shape[2]
                 nc.scalar.copy(
-                    grouped[:, h * HALF : (h + 1) * HALF, :].rearrange("p (c i) t -> p c t i", i=RUN),
+                    grouped[:, c0 : c0 + n, :].rearrange("p (c i) t -> p c t i", i=RUN),
                     raw[:].rearrange("p t (c i) -> p c t i", i=RUN),
                 )
+                c0 = c0 + n
+            return grouped
+
+        def quantise(grouped, fmt, name):
+            width = grouped.shape[1]
+            codes = keep.tile([P, width], U32, name=name + "_codes", align_bytes=64)
+            scales = keep.tile([P, width], U8, name=name + "_scales", align_bytes=64)
             nc.vector.quantize_mx(
-                out=codes[:].bitcast(fmt), scales=scales[:], in_=grouped[:].rearrange("p c t -> p (c t)")
+                out=codes[:].bitcast(fmt), scales=scales[:], in_=grouped.rearrange("p c t -> p (c t)")
             )
             return codes, scales
 
-        def products(h, w_codes, w_scales):
-            for j in range(HALF // P):
-                b = h * (HALF // P) + j
-                cols = slice(j * P, (j + 1) * P)
-                bank = psum.tile([P, X], F32, name=f"bank{b}")
-                nc.tensor.matmul_mx(
-                    out=bank[:],
-                    lhsT=w_codes[:, cols].bitcast(E4M3X4),
-                    lhsT_scale=w_scales[:, cols],
-                    rhs=dy_codes[:].bitcast(E5M2X4),
-                    rhs_scale=dy_scales[:],
-                    start=True,
-                    stop=True,
-                )
-                nc.scalar.copy(u_win[b][:, 0:X], bank[:])
+        u_win = {}
+
+        def product(b, w_codes, w_scales, j, tag):
+            cols = slice(j * P, (j + 1) * P)
+            bank = psum.tile([P, X], F32, name=f"bank{b}")
+            nc.tensor.matmul_mx(
+                out=bank[:],
+                lhsT=w_codes[:, cols].bitcast(E4M3X4),
+                lhsT_scale=w_scales[:, cols],
+                rhs=dy_codes[:].bitcast(E5M2X4),
+                rhs_scale=dy_scales[:],
+                start=True,
+                stop=True,
+            )
+            win = keep.tile([P, max(X, *PIECES[b]) + ENTRIES_PER_COLUMN], F32, name=f"u_win{b}", tag=tag)
+            nc.scalar.copy(win[:, 0:X], bank[:])
+            u_win.setdefault(b, win)
 
         def finish(b):
             c0 = 0
@@ -108,10 +122,16 @@ def tile_attend_gcfconv_f_kernel(tc, W, dyT, xT, soffs, toffs, out):
                 c0 = c0 + n
 
         xs = [gather_x(b, f"xs{b}") for b in range(BLOCKS - 1)]
-        dy_codes, dy_scales = quantise(dy_raw, E5M2X4, "dy")
-        w_first = quantise(w_raw[0:1], E4M3X4, "w0")
-        xs.append(gather_x(BLOCKS - 1, "w_raw0"))
-        products(0, *w_first)
-        products(1, *quantise(w_raw[1:2], E4M3X4, "w1"))
+        dy_codes, dy_scales = quantise(cast(dy_raw, "dy")[:], E5M2X4, "dy")
+        w0 = quantise(cast([w_head], "w0")[:], E4M3X4, "w0")
+        xs.append(gather_x(BLOCKS - 1, "w_head"))
+        mid = cast([w_mid], "w12")
+        tail = cast([w_tail], "w3")
+        product(0, *w0, 0, "w_tail")
+        w12 = quantise(mid[:], E4M3X4, "w12")
+        w3 = quantise(tail[:], E4M3X4, "w3")
+        product(1, *w12, 0, "u_win1")
+        product(2, *w12, 1, "u_win2")
+        product(3, *w3, 0, "u_win3")
         for b in range(BLOCKS):
             finish(b)

@@ -20,6 +20,9 @@ BLOCKS = D // P
 HALF = 256
 RUN = 4
 
+REGION = 48 * 1024
+SLOT = 8 * 1024
+
 X_WINDOW = 1376
 LAST_PIECES = (576, 288, 160)
 PIECES = [(C,)] * (BLOCKS - 1) + [LAST_PIECES]
@@ -29,20 +32,21 @@ def tile_attend_gcfconv_f_kernel(tc, W, dyT, xT, soffs, toffs, out):
     nc = tc.nc
     with ExitStack() as ctx:
         keep = ctx.enter_context(tc.tile_pool(name="keep", bufs=1))
+        far = ctx.enter_context(tc.tile_pool(name="far", bufs=1))
         psum = ctx.enter_context(tc.psum_pool(name="psum", bufs=1))
 
         src = keep.tile([P, C // ENTRIES_PER_COLUMN], U16, name="src")
         dst = keep.tile([P, C // ENTRIES_PER_COLUMN], U16, name="dst")
 
-        x_first = keep.tile([P, X_WINDOW], F32, name="x_first")
-        x_pair = keep.tile([P, X + X_WINDOW], F32, name="x_pair")
-        x_last = keep.tile([P, X_WINDOW], F32, name="x_last")
+        x_first = far.tile([P, X_WINDOW], F32, name="x_first", offset=REGION)
+        x_pair = far.tile([P, X + X_WINDOW], F32, name="x_pair", offset=REGION + SLOT)
+        x_last = far.tile([P, X_WINDOW], F32, name="x_last", offset=REGION + 2 * SLOT)
         x_win = [x_first[:], x_pair[:, 0:X_WINDOW], x_pair[:, X:], x_last[:]]
         dy_raw = [keep.tile([P, PACK, HALF], F32, name=f"dy_raw{h}") for h in range(2)]
         dy_rows = dyT.rearrange("(p t) x -> p t x", t=PACK)
-        w_head = keep.tile([P, PACK, P], F32, name="w_head")
+        w_head = far.tile([P, PACK, P], F32, name="w_head", offset=3 * SLOT)
         w_mid = keep.tile([P, PACK, HALF], F32, name="w_mid")
-        w_tail = keep.tile([P, PACK, P], F32, name="w_tail")
+        w_tail = far.tile([P, PACK, P], F32, name="w_tail", offset=2 * REGION)
         w_rows = W.rearrange("(p t) d -> p t d", t=PACK)
 
         def load_x(b):
@@ -65,8 +69,8 @@ def tile_attend_gcfconv_f_kernel(tc, W, dyT, xT, soffs, toffs, out):
         nc.sync.dma_start(w_tail[:], w_rows[:, :, P + HALF : D])
         nc.sync.dma_start(dst[:], toffs)
 
-        def gather_x(b, tag):
-            xs = keep.tile([P, C], F32, name=f"xs{b}", tag=tag)
+        def gather_x(b):
+            xs = far.tile([P, C], F32, name=f"xs{b}", offset=b * SLOT)
             nc.vector.tensor_copy(xs[:], x_win[b].indirect(src[:]))
             return xs
 
@@ -94,7 +98,7 @@ def tile_attend_gcfconv_f_kernel(tc, W, dyT, xT, soffs, toffs, out):
 
         u_win = {}
 
-        def product(b, w_codes, w_scales, j, tag):
+        def product(b, w_codes, w_scales, j):
             cols = slice(j * P, (j + 1) * P)
             bank = psum.tile([P, X], F32, name=f"bank{b}")
             nc.tensor.matmul_mx(
@@ -106,7 +110,8 @@ def tile_attend_gcfconv_f_kernel(tc, W, dyT, xT, soffs, toffs, out):
                 start=True,
                 stop=True,
             )
-            win = keep.tile([P, max(X, *PIECES[b]) + ENTRIES_PER_COLUMN], F32, name=f"u_win{b}", tag=tag)
+            width = max(X, *PIECES[b]) + ENTRIES_PER_COLUMN
+            win = far.tile([P, width], F32, name=f"u_win{b}", offset=2 * REGION + b * SLOT)
             nc.scalar.copy(win[:, 0:X], bank[:])
             u_win.setdefault(b, win)
 
@@ -114,24 +119,24 @@ def tile_attend_gcfconv_f_kernel(tc, W, dyT, xT, soffs, toffs, out):
             c0 = 0
             for n in PIECES[b]:
                 entries = dst[:, c0 // ENTRIES_PER_COLUMN : (c0 + n) // ENTRIES_PER_COLUMN]
-                res = keep.tile([P, n], F32, name=f"res{b}_{c0}")
+                res = far.tile([P, n], F32, name=f"res{b}_{c0}", offset=3 * REGION + b * SLOT + 4 * c0)
                 nc.vector.tensor_tensor(
                     res[:], u_win[b][:].indirect(entries), xs[b][:, c0 : c0 + n], mybir.AluOpType.mult
                 )
                 nc.sync.dma_start(out[b * P : (b + 1) * P, c0 : c0 + n], res[:])
                 c0 = c0 + n
 
-        xs = [gather_x(b, f"xs{b}") for b in range(BLOCKS - 1)]
+        xs = [gather_x(b) for b in range(BLOCKS - 1)]
         dy_codes, dy_scales = quantise(cast(dy_raw, "dy")[:], E5M2X4, "dy")
         w0 = quantise(cast([w_head], "w0")[:], E4M3X4, "w0")
-        xs.append(gather_x(BLOCKS - 1, "w_head"))
+        xs.append(gather_x(BLOCKS - 1))
         mid = cast([w_mid], "w12")
         tail = cast([w_tail], "w3")
-        product(0, *w0, 0, "w_tail")
+        product(0, *w0, 0)
         w12 = quantise(mid[:], E4M3X4, "w12")
         w3 = quantise(tail[:], E4M3X4, "w3")
-        product(1, *w12, 0, "u_win1")
-        product(2, *w12, 1, "u_win2")
-        product(3, *w3, 0, "u_win3")
+        product(1, *w12, 0)
+        product(2, *w12, 1)
+        product(3, *w3, 0)
         for b in range(BLOCKS):
             finish(b)

@@ -24,7 +24,7 @@ REGION = 48 * 1024
 SLOT = 8 * 1024
 
 X_WINDOW = 1376
-LAST_PIECES = (576, 288, 160)
+LAST_PIECES = (512, 320, 192)
 PIECES = [(C,)] * (BLOCKS - 1) + [LAST_PIECES]
 
 

@@ -24,6 +24,7 @@ REGION = 48 * 1024
 SLOT = 8 * 1024
 
 X_WINDOW = 1376
+FIRST_WINDOW = 2304
 LAST_PIECES = (512, 320, 192)
 PIECES = [(C,)] * (BLOCKS - 1) + [LAST_PIECES]
 
@@ -38,39 +39,35 @@ def tile_attend_gcfconv_f_kernel(tc, W, dyT, xT, soffs, toffs, out):
         src = keep.tile([P, C // ENTRIES_PER_COLUMN], U16, name="src")
         dst = keep.tile([P, C // ENTRIES_PER_COLUMN], U16, name="dst")
 
-        x_first = far.tile([P, X_WINDOW], F32, name="x_first", offset=REGION)
-        x_pair = far.tile([P, X + X_WINDOW], F32, name="x_pair", offset=REGION + SLOT)
-        x_last = far.tile([P, X_WINDOW], F32, name="x_last", offset=REGION + 2 * SLOT)
+        x_first = far.tile([P, FIRST_WINDOW], F32, name="x_first", offset=REGION)
+        x_pair = far.tile([P, X + X_WINDOW], F32, name="x_pair", offset=REGION + 3 * SLOT)
+        x_last = far.tile([P, X_WINDOW], F32, name="x_last", offset=REGION + 32 - 4 * X_WINDOW)
         x_win = [x_first[:], x_pair[:, 0:X_WINDOW], x_pair[:, X:], x_last[:]]
         dy_raw = [keep.tile([P, PACK, HALF], F32, name=f"dy_raw{h}") for h in range(2)]
         dy_rows = dyT.rearrange("(p t) x -> p t x", t=PACK)
-        w_head = far.tile([P, PACK, P], F32, name="w_head", offset=3 * SLOT)
-        w_mid = keep.tile([P, PACK, HALF], F32, name="w_mid")
-        w_tail = far.tile([P, PACK, P], F32, name="w_tail", offset=2 * REGION)
+        w_head = far.tile([P, PACK, P], F32, name="w_head", offset=REGION + 32)
+        w_mid = far.tile([P, PACK, HALF], F32, name="w_mid", offset=REGION + 32 + 4 * C)
+        w_tail = far.tile([P, PACK, P], F32, name="w_tail", offset=REGION + 32 + 8 * C)
         w_rows = W.rearrange("(p t) d -> p t d", t=PACK)
 
-        def load_x(b):
-            nc.sync.dma_start(x_win[b][:, 0:X], xT[b * P : (b + 1) * P, :])
+        def load_x(b, queue):
+            queue.dma_start(x_win[b][:, 0:X], xT[b * P : (b + 1) * P, :])
 
         def load_half(raw, rows, h):
-            nc.sync.dma_start(raw[h][:], rows[:, :, h * HALF : (h + 1) * HALF])
+            nc.scalar.dma_start(raw[h][:], rows[:, :, h * HALF : (h + 1) * HALF])
 
-        load_x(0)
+        load_x(0, nc.scalar)
         nc.sync.dma_start(src[:], soffs)
-        nc.sync.dma_start(
+        nc.sync.dma_start(dst[:], toffs)
+        nc.scalar.dma_start(
             x_pair[:, 0 : 2 * X].rearrange("p (b x) -> p b x", b=2),
             xT[P : 3 * P, :].rearrange("(b p) x -> p b x", b=2),
         )
         load_half(dy_raw, dy_rows, 0)
         load_half(dy_raw, dy_rows, 1)
-        nc.sync.dma_start(w_head[:], w_rows[:, :, 0:P])
-        load_x(3)
-        nc.sync.dma_start(w_mid[:], w_rows[:, :, P : P + HALF])
-        nc.sync.dma_start(w_tail[:], w_rows[:, :, P + HALF : D])
-        nc.sync.dma_start(dst[:], toffs)
 
         def gather_x(b):
-            xs = far.tile([P, C], F32, name=f"xs{b}", offset=b * SLOT)
+            xs = far.tile([P, C], F32, name=f"xs{b}", offset=b * SLOT if b < BLOCKS - 1 else REGION + 32)
             nc.vector.tensor_copy(xs[:], x_win[b].indirect(src[:]))
             return xs
 
@@ -111,7 +108,7 @@ def tile_attend_gcfconv_f_kernel(tc, W, dyT, xT, soffs, toffs, out):
                 stop=True,
             )
             width = max(X, *PIECES[b]) + ENTRIES_PER_COLUMN
-            win = far.tile([P, width], F32, name=f"u_win{b}", offset=2 * REGION + b * SLOT)
+            win = far.tile([P, width], F32, name=f"u_win{b}", offset=2 * REGION + b * SLOT if b else REGION + 32 + 8 * C)
             nc.scalar.copy(win[:, 0:X], bank[:])
             u_win.setdefault(b, win)
 
@@ -127,6 +124,10 @@ def tile_attend_gcfconv_f_kernel(tc, W, dyT, xT, soffs, toffs, out):
                 c0 = c0 + n
 
         xs = [gather_x(b) for b in range(BLOCKS - 1)]
+        nc.sync.dma_start(w_head[:], w_rows[:, :, 0:P])
+        load_x(3, nc.sync)
+        nc.sync.dma_start(w_mid[:], w_rows[:, :, P : P + HALF])
+        nc.sync.dma_start(w_tail[:], w_rows[:, :, P + HALF : D])
         dy_codes, dy_scales = quantise(cast(dy_raw, "dy")[:], E5M2X4, "dy")
         w0 = quantise(cast([w_head], "w0")[:], E4M3X4, "w0")
         xs.append(gather_x(BLOCKS - 1))

@@ -19,69 +19,57 @@ ENTRIES_PER_COLUMN = 16
 BLOCKS = D // P
 HALF = 256
 RUN = 4
-
-REGION = 48 * 1024
-SLOT = 8 * 1024
-
 X_WINDOW = 1376
-FIRST_WINDOW = 2304
 LAST_PIECES = (512, 320, 192)
-PIECES = [(C,)] * (BLOCKS - 1) + [LAST_PIECES]
 
 
 def tile_attend_gcfconv_f_kernel(tc, W, dyT, xT, soffs, toffs, out):
     nc = tc.nc
     with ExitStack() as ctx:
         keep = ctx.enter_context(tc.tile_pool(name="keep", bufs=1))
-        far = ctx.enter_context(tc.tile_pool(name="far", bufs=1))
         psum = ctx.enter_context(tc.psum_pool(name="psum", bufs=1))
 
         src = keep.tile([P, C // ENTRIES_PER_COLUMN], U16, name="src")
         dst = keep.tile([P, C // ENTRIES_PER_COLUMN], U16, name="dst")
+        x_all = keep.tile([P, (BLOCKS - 1) * X + X_WINDOW], F32, name="x_all")
+        order = list(reversed(range(BLOCKS)))
 
-        x_first = far.tile([P, FIRST_WINDOW], F32, name="x_first", offset=REGION)
-        x_pair = far.tile([P, X + X_WINDOW], F32, name="x_pair", offset=REGION + 3 * SLOT)
-        x_last = far.tile([P, X_WINDOW], F32, name="x_last", offset=REGION + 32 - 4 * X_WINDOW)
-        x_win = [x_first[:], x_pair[:, 0:X_WINDOW], x_pair[:, X:], x_last[:]]
-        dy_raw = [keep.tile([P, PACK, HALF], F32, name=f"dy_raw{h}") for h in range(2)]
-        dy_rows = dyT.rearrange("(p t) x -> p t x", t=PACK)
-        w_head = far.tile([P, PACK, P], F32, name="w_head", offset=REGION + 32)
-        w_mid = far.tile([P, PACK, HALF], F32, name="w_mid", offset=REGION + 32 + 4 * C)
-        w_tail = far.tile([P, PACK, P], F32, name="w_tail", offset=REGION + 32 + 8 * C)
-        w_rows = W.rearrange("(p t) d -> p t d", t=PACK)
+        def load_x(b0, b1):
+            n = b1 - b0
+            nc.scalar.dma_start(
+                x_all[:, b0 * X : b1 * X].rearrange("p (b x) -> p b x", b=n),
+                xT[b0 * P : b1 * P, :].rearrange("(b p) x -> p b x", b=n),
+            )
 
-        def load_x(b, queue):
-            queue.dma_start(x_win[b][:, 0:X], xT[b * P : (b + 1) * P, :])
+        def load_halves(mat, name):
+            rows = mat.rearrange("(p t) c -> p t c", t=PACK)
+            raws = []
+            for h in range(2):
+                raw = keep.tile([P, PACK, HALF], F32, name=f"{name}_raw{h}", tag=f"{name}_raw{h}")
+                nc.scalar.dma_start(raw[:], rows[:, :, h * HALF : (h + 1) * HALF])
+                raws.append(raw)
+            return raws
 
-        def load_half(raw, rows, h):
-            nc.scalar.dma_start(raw[h][:], rows[:, :, h * HALF : (h + 1) * HALF])
-
-        load_x(0, nc.scalar)
+        load_x(3, 4)
         nc.sync.dma_start(src[:], soffs)
         nc.sync.dma_start(dst[:], toffs)
-        nc.scalar.dma_start(
-            x_pair[:, 0 : 2 * X].rearrange("p (b x) -> p b x", b=2),
-            xT[P : 3 * P, :].rearrange("(b p) x -> p b x", b=2),
-        )
-        load_half(dy_raw, dy_rows, 0)
-        load_half(dy_raw, dy_rows, 1)
+        load_x(1, 3)
+        dy_raw = load_halves(dyT, "dy")
+        w_raw = load_halves(W, "w")
+        load_x(0, 1)
 
         def gather_x(b):
-            xs = far.tile([P, C], F32, name=f"xs{b}", offset=b * SLOT if b < BLOCKS - 1 else REGION + 32)
-            nc.vector.tensor_copy(xs[:], x_win[b].indirect(src[:]))
+            xs = keep.tile([P, C], F32, name=f"xs{b}", tag="w_raw1" if b == order[-1] else f"xs{b}")
+            nc.vector.tensor_copy(xs[:], x_all[:, b * X : b * X + X_WINDOW].indirect(src[:]))
             return xs
 
         def cast(raws, name):
-            width = sum(raw[:].shape[2] for raw in raws)
-            grouped = keep.tile([P, width, PACK], BF16, name=name + "_grouped", align_bytes=64)
-            c0 = 0
-            for raw in raws:
-                n = raw[:].shape[2]
+            grouped = keep.tile([P, 2 * HALF, PACK], BF16, name=name + "_grouped", align_bytes=64)
+            for h, raw in enumerate(raws):
                 nc.scalar.copy(
-                    grouped[:, c0 : c0 + n, :].rearrange("p (c i) t -> p c t i", i=RUN),
+                    grouped[:, h * HALF : (h + 1) * HALF, :].rearrange("p (c i) t -> p c t i", i=RUN),
                     raw[:].rearrange("p t (c i) -> p c t i", i=RUN),
                 )
-                c0 = c0 + n
             return grouped
 
         def quantise(grouped, fmt, name):
@@ -93,10 +81,15 @@ def tile_attend_gcfconv_f_kernel(tc, W, dyT, xT, soffs, toffs, out):
             )
             return codes, scales
 
-        u_win = {}
+        xs = {b: gather_x(b) for b in order[:-1]}
+        dy_codes, dy_scales = quantise(cast(dy_raw, "dy")[:], E5M2X4, "dy")
+        w_codes, w_scales = quantise(cast(w_raw, "w")[:], E4M3X4, "w")
+        xs.setdefault(order[-1], gather_x(order[-1]))
 
-        def product(b, w_codes, w_scales, j):
-            cols = slice(j * P, (j + 1) * P)
+        pieces = {b: LAST_PIECES if b == order[-1] else (C,) for b in order}
+        u_win = {}
+        for b in order:
+            cols = slice(b * P, (b + 1) * P)
             bank = psum.tile([P, X], F32, name=f"bank{b}")
             nc.tensor.matmul_mx(
                 out=bank[:],
@@ -107,37 +100,19 @@ def tile_attend_gcfconv_f_kernel(tc, W, dyT, xT, soffs, toffs, out):
                 start=True,
                 stop=True,
             )
-            width = max(X, *PIECES[b]) + ENTRIES_PER_COLUMN
-            win = far.tile([P, width], F32, name=f"u_win{b}", offset=2 * REGION + b * SLOT if b else REGION + 32 + 8 * C)
+            win = keep.tile([P, max(X, *pieces[b]) + ENTRIES_PER_COLUMN], F32, name=f"u_win{b}")
             nc.scalar.copy(win[:, 0:X], bank[:])
             u_win.setdefault(b, win)
 
-        def finish(b):
+        for b in order:
             c0 = 0
-            for n in PIECES[b]:
+            for n in pieces[b]:
                 entries = dst[:, c0 // ENTRIES_PER_COLUMN : (c0 + n) // ENTRIES_PER_COLUMN]
-                res = far.tile([P, n], F32, name=f"res{b}_{c0}", offset=3 * REGION + b * SLOT + 4 * c0)
+                res = keep.tile([P, n], F32, name=f"res{b}_{c0}")
                 nc.vector.tensor_tensor(
                     res[:], u_win[b][:].indirect(entries), xs[b][:, c0 : c0 + n], mybir.AluOpType.mult
                 )
-                nc.sync.dma_start(out[b * P : (b + 1) * P, c0 : c0 + n], res[:])
+                step = n // 2 if b == order[0] else n
+                for s in range(0, n, step):
+                    nc.sync.dma_start(out[b * P : (b + 1) * P, c0 + s : c0 + s + step], res[:, s : s + step])
                 c0 = c0 + n
-
-        xs = [gather_x(b) for b in range(BLOCKS - 1)]
-        nc.sync.dma_start(w_head[:], w_rows[:, :, 0:P])
-        load_x(3, nc.sync)
-        nc.sync.dma_start(w_mid[:], w_rows[:, :, P : P + HALF])
-        nc.sync.dma_start(w_tail[:], w_rows[:, :, P + HALF : D])
-        dy_codes, dy_scales = quantise(cast(dy_raw, "dy")[:], E5M2X4, "dy")
-        w0 = quantise(cast([w_head], "w0")[:], E4M3X4, "w0")
-        xs.append(gather_x(BLOCKS - 1))
-        mid = cast([w_mid], "w12")
-        tail = cast([w_tail], "w3")
-        product(0, *w0, 0)
-        w12 = quantise(mid[:], E4M3X4, "w12")
-        w3 = quantise(tail[:], E4M3X4, "w3")
-        product(1, *w12, 0)
-        product(2, *w12, 1)
-        product(3, *w3, 0)
-        for b in range(BLOCKS):
-            finish(b)

@@ -56,11 +56,12 @@ def tile_attend_gcfconv_f_kernel(tc, W, dyT, xT, soffs, toffs, out):
         load_x(1, 3)
         dy_raw = load_halves(dyT, "dy")
         w_raw = load_halves(W, "w")
-        load_x(0, 1)
+        x_late = keep.tile([P, X_WINDOW], F32, name="x_late", tag="dy_raw0")
 
         def gather_x(b):
             xs = keep.tile([P, C], F32, name=f"xs{b}", tag="w_raw1" if b == order[-1] else f"xs{b}")
-            nc.vector.tensor_copy(xs[:], x_all[:, b * X : b * X + X_WINDOW].indirect(src[:]))
+            win = x_all[:, b * X : b * X + X_WINDOW] if b else x_late[:]
+            nc.vector.tensor_copy(xs[:], win.indirect(src[:]))
             return xs
 
         def cast(raws, name):
@@ -83,6 +84,7 @@ def tile_attend_gcfconv_f_kernel(tc, W, dyT, xT, soffs, toffs, out):
 
         xs = {b: gather_x(b) for b in order[:-1]}
         dy_codes, dy_scales = quantise(cast(dy_raw, "dy")[:], E5M2X4, "dy")
+        nc.sync.dma_start(x_late[:, 0:X], xT[0:P, :])
         w_codes, w_scales = quantise(cast(w_raw, "w")[:], E4M3X4, "w")
         xs.setdefault(order[-1], gather_x(order[-1]))
 

@@ -55,20 +55,23 @@ def tile_attend_gcfconv_f_kernel(tc, W, dyT, xT, soffs, toffs, out):
         nc.sync.dma_start(dst[:], toffs)
         load_x(1, 3)
         dy_raw = load_halves(dyT, "dy")
-        w_raw = load_halves(W, "w")
-        x_late = keep.tile([P, X_WINDOW], F32, name="x_late", tag="dy_raw0")
+        w_rows = W.rearrange("(p t) c -> p t c", t=PACK)
+        w_first = keep.tile([P, PACK, P], F32, name="w_first", tag="w_first")
+        nc.scalar.dma_start(w_first[:], w_rows[:, :, 3 * P : D])
+        load_x(0, 1)
 
         def gather_x(b):
-            xs = keep.tile([P, C], F32, name=f"xs{b}", tag="w_raw1" if b == order[-1] else f"xs{b}")
-            win = x_all[:, b * X : b * X + X_WINDOW] if b else x_late[:]
+            xs = keep.tile([P, C], F32, name=f"xs{b}", tag="w_first" if b == order[-1] else f"xs{b}")
+            win = x_all[:, b * X : b * X + X_WINDOW]
             nc.vector.tensor_copy(xs[:], win.indirect(src[:]))
             return xs
 
         def cast(raws, name):
-            grouped = keep.tile([P, 2 * HALF, PACK], BF16, name=name + "_grouped", align_bytes=64)
+            n = raws[0][:].shape[2]
+            grouped = keep.tile([P, len(raws) * n, PACK], BF16, name=name + "_grouped", align_bytes=64)
             for h, raw in enumerate(raws):
                 nc.scalar.copy(
-                    grouped[:, h * HALF : (h + 1) * HALF, :].rearrange("p (c i) t -> p c t i", i=RUN),
+                    grouped[:, h * n : (h + 1) * n, :].rearrange("p (c i) t -> p c t i", i=RUN),
                     raw[:].rearrange("p t (c i) -> p c t i", i=RUN),
                 )
             return grouped
@@ -84,14 +87,21 @@ def tile_attend_gcfconv_f_kernel(tc, W, dyT, xT, soffs, toffs, out):
 
         xs = {b: gather_x(b) for b in order[:-1]}
         dy_codes, dy_scales = quantise(cast(dy_raw, "dy")[:], E5M2X4, "dy")
-        nc.sync.dma_start(x_late[:, 0:X], xT[0:P, :])
-        w_codes, w_scales = quantise(cast(w_raw, "w")[:], E4M3X4, "w")
+        w_mid = keep.tile([P, PACK, HALF], F32, name="w_mid", tag="dy_raw0")
+        w_last = keep.tile([P, PACK, P], F32, name="w_last", tag="dy_raw1")
+        nc.sync.dma_start(w_mid[:], w_rows[:, :, P : 3 * P])
+        nc.sync.dma_start(w_last[:], w_rows[:, :, 0:P])
+        q_first = quantise(cast([w_first], "w_first")[:], E4M3X4, "w_first")
         xs.setdefault(order[-1], gather_x(order[-1]))
+        q_mid = quantise(cast([w_mid], "w_mid")[:], E4M3X4, "w_mid")
+        q_last = quantise(cast([w_last], "w_last")[:], E4M3X4, "w_last")
+        w_parts = {3: (q_first, 0), 2: (q_mid, 1), 1: (q_mid, 0), 0: (q_last, 0)}
 
         pieces = {b: LAST_PIECES if b == order[-1] else (C,) for b in order}
         u_win = {}
         for b in order:
-            cols = slice(b * P, (b + 1) * P)
+            (w_codes, w_scales), j = w_parts[b]
+            cols = slice(j * P, (j + 1) * P)
             bank = psum.tile([P, X], F32, name=f"bank{b}")
             nc.tensor.matmul_mx(
                 out=bank[:],
@@ -102,7 +112,8 @@ def tile_attend_gcfconv_f_kernel(tc, W, dyT, xT, soffs, toffs, out):
                 start=True,
                 stop=True,
             )
-            win = keep.tile([P, max(X, *pieces[b]) + ENTRIES_PER_COLUMN], F32, name=f"u_win{b}")
+            win = keep.tile([P, max(X, *pieces[b]) + ENTRIES_PER_COLUMN], F32, name=f"u_win{b}",
+                            tag="dy_raw1" if b == order[0] else f"u_win{b}")
             nc.scalar.copy(win[:, 0:X], bank[:])
             u_win.setdefault(b, win)
 
@@ -114,7 +125,5 @@ def tile_attend_gcfconv_f_kernel(tc, W, dyT, xT, soffs, toffs, out):
                 nc.vector.tensor_tensor(
                     res[:], u_win[b][:].indirect(entries), xs[b][:, c0 : c0 + n], mybir.AluOpType.mult
                 )
-                step = n // 2 if b == order[0] else n
-                for s in range(0, n, step):
-                    nc.sync.dma_start(out[b * P : (b + 1) * P, c0 + s : c0 + s + step], res[:, s : s + step])
+                nc.sync.dma_start(out[b * P : (b + 1) * P, c0 : c0 + n], res[:])
                 c0 = c0 + n

@@ -59,6 +59,10 @@ def tile_attend_gcfconv_f_kernel(tc, W, dyT, xT, soffs, toffs, out):
         w_first = keep.tile([P, PACK, P], F32, name="w_first", tag="w_first")
         nc.scalar.dma_start(w_first[:], w_rows[:, :, 3 * P : D])
         load_x(0, 1)
+        w_mid = keep.tile([P, PACK, HALF], F32, name="w_mid")
+        w_last = keep.tile([P, PACK, P], F32, name="w_last", tag="w_last")
+        nc.scalar.dma_start(w_mid[:], w_rows[:, :, P : 3 * P])
+        nc.scalar.dma_start(w_last[:], w_rows[:, :, 0:P])
 
         def gather_x(b):
             xs = keep.tile([P, C], F32, name=f"xs{b}", tag="w_first" if b == order[-1] else f"xs{b}")
@@ -87,10 +91,6 @@ def tile_attend_gcfconv_f_kernel(tc, W, dyT, xT, soffs, toffs, out):
 
         xs = {b: gather_x(b) for b in order[:-1]}
         dy_codes, dy_scales = quantise(cast(dy_raw, "dy")[:], E5M2X4, "dy")
-        w_mid = keep.tile([P, PACK, HALF], F32, name="w_mid", tag="dy_raw0")
-        w_last = keep.tile([P, PACK, P], F32, name="w_last", tag="dy_raw1")
-        nc.sync.dma_start(w_mid[:], w_rows[:, :, P : 3 * P])
-        nc.sync.dma_start(w_last[:], w_rows[:, :, 0:P])
         q_first = quantise(cast([w_first], "w_first")[:], E4M3X4, "w_first")
         xs.setdefault(order[-1], gather_x(order[-1]))
         q_mid = quantise(cast([w_mid], "w_mid")[:], E4M3X4, "w_mid")
@@ -113,7 +113,7 @@ def tile_attend_gcfconv_f_kernel(tc, W, dyT, xT, soffs, toffs, out):
                 stop=True,
             )
             win = keep.tile([P, max(X, *pieces[b]) + ENTRIES_PER_COLUMN], F32, name=f"u_win{b}",
-                            tag="dy_raw1" if b == order[0] else f"u_win{b}")
+                            tag="w_last" if b == order[0] else f"u_win{b}")
             nc.scalar.copy(win[:, 0:X], bank[:])
             u_win.setdefault(b, win)
 

@@ -19,6 +19,7 @@ ENTRIES_PER_COLUMN = 16
 BLOCKS = D // P
 HALF = 256
 RUN = 4
+STRETCH = 32 * 1024
 X_WINDOW = 1376
 LAST_PIECES = (512, 320, 192)
 
@@ -27,19 +28,17 @@ def tile_attend_gcfconv_f_kernel(tc, W, dyT, xT, soffs, toffs, out):
     nc = tc.nc
     with ExitStack() as ctx:
         keep = ctx.enter_context(tc.tile_pool(name="keep", bufs=1))
+        far = ctx.enter_context(tc.tile_pool(name="far", bufs=1))
         psum = ctx.enter_context(tc.psum_pool(name="psum", bufs=1))
 
         src = keep.tile([P, C // ENTRIES_PER_COLUMN], U16, name="src")
         dst = keep.tile([P, C // ENTRIES_PER_COLUMN], U16, name="dst")
-        x_all = keep.tile([P, (BLOCKS - 1) * X + X_WINDOW], F32, name="x_all")
         order = list(reversed(range(BLOCKS)))
-
-        def load_x(b0, b1):
-            n = b1 - b0
-            nc.scalar.dma_start(
-                x_all[:, b0 * X : b1 * X].rearrange("p (b x) -> p b x", b=n),
-                xT[b0 * P : b1 * P, :].rearrange("(b p) x -> p b x", b=n),
-            )
+        place = {b: (BLOCKS - b if b in (0, 3) else b + 1) * STRETCH - 2 * X for b in order}
+        x_first = far.tile([P, X_WINDOW], F32, name="x_first", offset=place[3])
+        x_pair = far.tile([P, 2, STRETCH // 4], F32, name="x_pair", offset=place[1])
+        x_late = far.tile([P, X_WINDOW], F32, name="x_late", offset=place[0])
+        x_win = {3: x_first[:], 2: x_pair[:, 1, 0:X_WINDOW], 1: x_pair[:, 0, 0:X_WINDOW], 0: x_late[:]}
 
         def load_halves(mat, name):
             rows = mat.rearrange("(p t) c -> p t c", t=PACK)
@@ -50,23 +49,23 @@ def tile_attend_gcfconv_f_kernel(tc, W, dyT, xT, soffs, toffs, out):
                 raws.append(raw)
             return raws
 
-        load_x(3, 4)
+        nc.scalar.dma_start(x_first[:, 0:X], xT[3 * P : D, :])
         nc.sync.dma_start(src[:], soffs)
         nc.sync.dma_start(dst[:], toffs)
-        load_x(1, 3)
+        nc.scalar.dma_start(x_pair[:, :, 0:X], xT[P : 3 * P, :].rearrange("(b p) x -> p b x", b=2))
         dy_raw = load_halves(dyT, "dy")
         w_rows = W.rearrange("(p t) c -> p t c", t=PACK)
         w_first = keep.tile([P, PACK, P], F32, name="w_first", tag="w_first")
         nc.scalar.dma_start(w_first[:], w_rows[:, :, 3 * P : D])
-        load_x(0, 1)
-        w_mid = keep.tile([P, PACK, HALF], F32, name="w_mid")
-        w_last = keep.tile([P, PACK, P], F32, name="w_last", tag="w_last")
+        nc.scalar.dma_start(x_late[:, 0:X], xT[0:P, :])
+        w_mid = far.tile([P, PACK, HALF], F32, name="w_mid", offset=0, align_bytes=STRETCH)
+        w_last = far.tile([P, PACK, P], F32, name="w_last", offset=place[3] + 4 * X_WINDOW)
         nc.scalar.dma_start(w_mid[:], w_rows[:, :, P : 3 * P])
         nc.scalar.dma_start(w_last[:], w_rows[:, :, 0:P])
 
         def gather_x(b):
             xs = keep.tile([P, C], F32, name=f"xs{b}", tag="w_first" if b == order[-1] else f"xs{b}")
-            win = x_all[:, b * X : b * X + X_WINDOW]
+            win = x_win[b]
             nc.vector.tensor_copy(xs[:], win.indirect(src[:]))
             return xs
 
@@ -112,8 +111,8 @@ def tile_attend_gcfconv_f_kernel(tc, W, dyT, xT, soffs, toffs, out):
                 start=True,
                 stop=True,
             )
-            win = keep.tile([P, max(X, *pieces[b]) + ENTRIES_PER_COLUMN], F32, name=f"u_win{b}",
-                            tag="w_last" if b == order[0] else f"u_win{b}")
+            width = 2 * C if b == order[0] else max(X, *pieces[b]) + ENTRIES_PER_COLUMN
+            win = far.tile([P, width], F32, name=f"u_win{b}", offset=place[b])
             nc.scalar.copy(win[:, 0:X], bank[:])
             u_win.setdefault(b, win)
 

@@ -20,6 +20,8 @@ BLOCKS = D // P
 HALF = 256
 RUN = 4
 STRETCH = 32 * 1024
+KIB = 1024
+FIRST_PIECE = 1024
 X_WINDOW = 1376
 LAST_PIECES = (512, 320, 192)
 
@@ -34,37 +36,40 @@ def tile_attend_gcfconv_f_kernel(tc, W, dyT, xT, soffs, toffs, out):
         src = keep.tile([P, C // ENTRIES_PER_COLUMN], U16, name="src")
         dst = keep.tile([P, C // ENTRIES_PER_COLUMN], U16, name="dst")
         order = list(reversed(range(BLOCKS)))
-        place = {b: (BLOCKS - b if b in (0, 3) else b + 1) * STRETCH - 2 * X for b in order}
-        x_first = far.tile([P, X_WINDOW], F32, name="x_first", offset=place[3])
-        x_pair = far.tile([P, 2, STRETCH // 4], F32, name="x_pair", offset=place[1])
-        x_late = far.tile([P, X_WINDOW], F32, name="x_late", offset=place[0])
+        x_at = {3: 3 * STRETCH, 1: 4 * STRETCH, 2: 5 * STRETCH, 0: 3 * STRETCH + 8 * KIB}
+        u_at = {3: 2 * STRETCH, 2: x_at[3], 1: x_at[1], 0: x_at[2]}
+        xs_at = {b: STRETCH + b * 4 * C for b in order}
+        res_at = {3: 16 * KIB, 2: u_at[3] + 8 * KIB, 1: 20 * KIB, 0: u_at[3] + 12 * KIB}
+        x_first = far.tile([P, X_WINDOW], F32, name="x_first", offset=x_at[3])
+        x_pair = far.tile([P, 2, STRETCH // 4], F32, name="x_pair", offset=x_at[1])
+        x_late = far.tile([P, X_WINDOW], F32, name="x_late", offset=x_at[0])
         x_win = {3: x_first[:], 2: x_pair[:, 1, 0:X_WINDOW], 1: x_pair[:, 0, 0:X_WINDOW], 0: x_late[:]}
 
         def load_halves(mat, name):
             rows = mat.rearrange("(p t) c -> p t c", t=PACK)
             raws = []
             for h in range(2):
-                raw = keep.tile([P, PACK, HALF], F32, name=f"{name}_raw{h}", tag=f"{name}_raw{h}")
+                raw = far.tile([P, PACK, HALF], F32, name=f"{name}_raw{h}", offset=(1 + h) * 4 * KIB)
                 nc.scalar.dma_start(raw[:], rows[:, :, h * HALF : (h + 1) * HALF])
                 raws.append(raw)
             return raws
 
-        nc.scalar.dma_start(x_first[:, 0:X], xT[3 * P : D, :])
+        nc.scalar.dma_start(x_first[:, 0:X], xT[3 * P : D, :], max_dma_last_dim=FIRST_PIECE)
         nc.sync.dma_start(src[:], soffs)
         nc.sync.dma_start(dst[:], toffs)
         nc.scalar.dma_start(x_pair[:, :, 0:X], xT[P : 3 * P, :].rearrange("(b p) x -> p b x", b=2))
         dy_raw = load_halves(dyT, "dy")
         w_rows = W.rearrange("(p t) c -> p t c", t=PACK)
-        w_first = keep.tile([P, PACK, P], F32, name="w_first", tag="w_first")
+        w_first = far.tile([P, PACK, P], F32, name="w_first", offset=xs_at[0])
         nc.scalar.dma_start(w_first[:], w_rows[:, :, 3 * P : D])
         nc.scalar.dma_start(x_late[:, 0:X], xT[0:P, :])
         w_mid = far.tile([P, PACK, HALF], F32, name="w_mid", offset=0, align_bytes=STRETCH)
-        w_last = far.tile([P, PACK, P], F32, name="w_last", offset=place[3] + 4 * X_WINDOW)
+        w_last = far.tile([P, PACK, P], F32, name="w_last", offset=u_at[3])
         nc.scalar.dma_start(w_mid[:], w_rows[:, :, P : 3 * P])
         nc.scalar.dma_start(w_last[:], w_rows[:, :, 0:P])
 
         def gather_x(b):
-            xs = keep.tile([P, C], F32, name=f"xs{b}", tag="w_first" if b == order[-1] else f"xs{b}")
+            xs = far.tile([P, C], F32, name=f"xs{b}", offset=xs_at[b])
             win = x_win[b]
             nc.vector.tensor_copy(xs[:], win.indirect(src[:]))
             return xs
@@ -111,8 +116,8 @@ def tile_attend_gcfconv_f_kernel(tc, W, dyT, xT, soffs, toffs, out):
                 start=True,
                 stop=True,
             )
-            width = 2 * C if b == order[0] else max(X, *pieces[b]) + ENTRIES_PER_COLUMN
-            win = far.tile([P, width], F32, name=f"u_win{b}", offset=place[b])
+            width = max(X, *pieces[b]) + ENTRIES_PER_COLUMN
+            win = far.tile([P, width], F32, name=f"u_win{b}", offset=u_at[b])
             nc.scalar.copy(win[:, 0:X], bank[:])
             u_win.setdefault(b, win)
 
@@ -120,7 +125,7 @@ def tile_attend_gcfconv_f_kernel(tc, W, dyT, xT, soffs, toffs, out):
             c0 = 0
             for n in pieces[b]:
                 entries = dst[:, c0 // ENTRIES_PER_COLUMN : (c0 + n) // ENTRIES_PER_COLUMN]
-                res = keep.tile([P, n], F32, name=f"res{b}_{c0}")
+                res = far.tile([P, n], F32, name=f"res{b}_{c0}", offset=res_at[b] + 4 * c0)
                 nc.vector.tensor_tensor(
                     res[:], u_win[b][:].indirect(entries), xs[b][:, c0 : c0 + n], mybir.AluOpType.mult
                 )

@@ -12,122 +12,129 @@ U16 = mybir.dt.uint16
 U8 = mybir.dt.uint8
 E4M3X4 = mybir.dt.float8_e4m3fn_x4
 E5M2X4 = mybir.dt.float8_e5m2_x4
+COPY = mybir.ActivationFunctionType.Copy
+MULT = mybir.AluOpType.mult
 
 P = 128
 PACK = 4
-ENTRIES_PER_COLUMN = 16
-BLOCKS = D // P
-HALF = 256
+PER_COLUMN = 16
 RUN = 4
-STRETCH = 32 * 1024
-KIB = 1024
-FIRST_PIECE = 1024
-X_WINDOW = 1376
-LAST_PIECES = (512, 320, 192)
+WINDOW = C + PER_COLUMN
+FIRST_WINDOW = 1376
+X_SPLIT = 640
 
 
 def tile_attend_gcfconv_f_kernel(tc, W, dyT, xT, soffs, toffs, out):
     nc = tc.nc
     with ExitStack() as ctx:
         keep = ctx.enter_context(tc.tile_pool(name="keep", bufs=1))
-        far = ctx.enter_context(tc.tile_pool(name="far", bufs=1))
         psum = ctx.enter_context(tc.psum_pool(name="psum", bufs=1))
 
-        src = keep.tile([P, C // ENTRIES_PER_COLUMN], U16, name="src")
-        dst = keep.tile([P, C // ENTRIES_PER_COLUMN], U16, name="dst")
-        order = list(reversed(range(BLOCKS)))
-        x_at = {3: 3 * STRETCH, 1: 4 * STRETCH, 2: 5 * STRETCH, 0: 3 * STRETCH + 8 * KIB}
-        u_at = {3: 2 * STRETCH, 2: x_at[3], 1: x_at[1], 0: x_at[2]}
-        xs_at = {b: STRETCH + b * 4 * C for b in order}
-        res_at = {3: 16 * KIB, 2: u_at[3] + 8 * KIB, 1: 20 * KIB, 0: u_at[3] + 12 * KIB}
-        x_first = far.tile([P, X_WINDOW], F32, name="x_first", offset=x_at[3])
-        x_pair = far.tile([P, 2, STRETCH // 4], F32, name="x_pair", offset=x_at[1])
-        x_late = far.tile([P, X_WINDOW], F32, name="x_late", offset=x_at[0])
-        x_win = {3: x_first[:], 2: x_pair[:, 1, 0:X_WINDOW], 1: x_pair[:, 0, 0:X_WINDOW], 0: x_late[:]}
+        src = keep.tile([P, C // PER_COLUMN], U16, name="src")
+        dst = keep.tile([P, C // PER_COLUMN], U16, name="dst")
 
-        def load_halves(mat, name):
-            rows = mat.rearrange("(p t) c -> p t c", t=PACK)
-            raws = []
-            for h in range(2):
-                raw = far.tile([P, PACK, HALF], F32, name=f"{name}_raw{h}", offset=(1 + h) * 4 * KIB)
-                nc.scalar.dma_start(raw[:], rows[:, :, h * HALF : (h + 1) * HALF])
-                raws.append(raw)
-            return raws
+        def entries(offsets, c0, c1):
+            return offsets[:, c0 // PER_COLUMN : c1 // PER_COLUMN]
 
-        nc.scalar.dma_start(x_first[:, 0:X], xT[3 * P : D, :], max_dma_last_dim=FIRST_PIECE)
+        def load_x(b, width):
+            win = keep.tile([P, width], F32, name=f"x_win{b}")
+            nc.sync.dma_start(win[:, 0:X], xT[b * P : (b + 1) * P, :])
+            return win
+
+        def load_operand(mat, c0, c1, name):
+            raw = keep.tile([P, PACK, c1 - c0], F32, name=name + "_raw")
+            nc.sync.dma_start(raw[:], mat.rearrange("(p t) c -> p t c", t=PACK)[:, :, c0:c1])
+            return raw
+
+        x_win = [load_x(0, FIRST_WINDOW)]
         nc.sync.dma_start(src[:], soffs)
+        w_raw0 = load_operand(W, 0, P, "w0")
+        x_win.append(load_x(1, WINDOW))
+        dy_raw0 = load_operand(dyT, 0, 2 * P, "dy0")
+        x_win.append(load_x(2, WINDOW))
+        x_win.append(load_x(3, WINDOW))
+        dy_raw1 = load_operand(dyT, 2 * P, X, "dy1")
+        w_raw1 = load_operand(W, P, 2 * P, "w1")
         nc.sync.dma_start(dst[:], toffs)
-        nc.scalar.dma_start(x_pair[:, :, 0:X], xT[P : 3 * P, :].rearrange("(b p) x -> p b x", b=2))
-        dy_raw = load_halves(dyT, "dy")
-        w_rows = W.rearrange("(p t) c -> p t c", t=PACK)
-        w_first = far.tile([P, PACK, P], F32, name="w_first", offset=xs_at[0])
-        nc.scalar.dma_start(w_first[:], w_rows[:, :, 3 * P : D])
-        nc.scalar.dma_start(x_late[:, 0:X], xT[0:P, :])
-        w_mid = far.tile([P, PACK, HALF], F32, name="w_mid", offset=0, align_bytes=STRETCH)
-        w_last = far.tile([P, PACK, P], F32, name="w_last", offset=u_at[3])
-        nc.scalar.dma_start(w_mid[:], w_rows[:, :, P : 3 * P])
-        nc.scalar.dma_start(w_last[:], w_rows[:, :, 0:P])
+        w_raw2 = load_operand(W, 2 * P, D, "w2")
 
-        def gather_x(b):
-            xs = far.tile([P, C], F32, name=f"xs{b}", offset=xs_at[b])
-            win = x_win[b]
-            nc.vector.tensor_copy(xs[:], win.indirect(src[:]))
-            return xs
+        xs = [keep.tile([P, C], F32, name=f"xs{b}") for b in range(4)]
+        ud = [keep.tile([P, C], F32, name=f"ud{b}") for b in range(4)]
+        codes = {n: keep.tile([P, X], U32, name=n + "_codes", align_bytes=64) for n in ("dy", "w")}
+        scales = {n: keep.tile([P, X], U8, name=n + "_scales", align_bytes=64) for n in ("dy", "w")}
+        fmt = {"dy": E5M2X4, "w": E4M3X4}
 
-        def cast(raws, name):
-            n = raws[0][:].shape[2]
-            grouped = keep.tile([P, len(raws) * n, PACK], BF16, name=name + "_grouped", align_bytes=64)
-            for h, raw in enumerate(raws):
-                nc.scalar.copy(
-                    grouped[:, h * n : (h + 1) * n, :].rearrange("p (c i) t -> p c t i", i=RUN),
-                    raw[:].rearrange("p t (c i) -> p c t i", i=RUN),
+        def prepare(raw, name, first, cast=nc.vector.tensor_copy):
+            blocks = raw[:].shape[2] // P
+            grouped = [
+                keep.tile([P, P, PACK], BF16, name=f"{name}_grouped{first + j}", align_bytes=64)
+                for j in range(blocks)
+            ]
+            for j in range(blocks):
+                cast(
+                    grouped[j][:].rearrange("p (c i) t -> p c t i", i=RUN),
+                    raw[:, :, j * P : (j + 1) * P].rearrange("p t (c i) -> p c t i", i=RUN),
                 )
-            return grouped
+            for j in range(blocks):
+                cols = slice((first + j) * P, (first + j + 1) * P)
+                nc.vector.quantize_mx(
+                    out=codes[name][:, cols].bitcast(fmt[name]),
+                    scales=scales[name][:, cols],
+                    in_=grouped[j][:].rearrange("p c t -> p (c t)"),
+                )
 
-        def quantise(grouped, fmt, name):
-            width = grouped.shape[1]
-            codes = keep.tile([P, width], U32, name=name + "_codes", align_bytes=64)
-            scales = keep.tile([P, width], U8, name=name + "_scales", align_bytes=64)
-            nc.vector.quantize_mx(
-                out=codes[:].bitcast(fmt), scales=scales[:], in_=grouped.rearrange("p c t -> p (c t)")
-            )
-            return codes, scales
-
-        xs = {b: gather_x(b) for b in order[:-1]}
-        dy_codes, dy_scales = quantise(cast(dy_raw, "dy")[:], E5M2X4, "dy")
-        q_first = quantise(cast([w_first], "w_first")[:], E4M3X4, "w_first")
-        xs.setdefault(order[-1], gather_x(order[-1]))
-        q_mid = quantise(cast([w_mid], "w_mid")[:], E4M3X4, "w_mid")
-        q_last = quantise(cast([w_last], "w_last")[:], E4M3X4, "w_last")
-        w_parts = {3: (q_first, 0), 2: (q_mid, 1), 1: (q_mid, 0), 0: (q_last, 0)}
-
-        pieces = {b: LAST_PIECES if b == order[-1] else (C,) for b in order}
-        u_win = {}
-        for b in order:
-            (w_codes, w_scales), j = w_parts[b]
-            cols = slice(j * P, (j + 1) * P)
+        def multiply(b):
+            cols = slice(b * P, (b + 1) * P)
             bank = psum.tile([P, X], F32, name=f"bank{b}")
             nc.tensor.matmul_mx(
                 out=bank[:],
-                lhsT=w_codes[:, cols].bitcast(E4M3X4),
-                lhsT_scale=w_scales[:, cols],
-                rhs=dy_codes[:].bitcast(E5M2X4),
-                rhs_scale=dy_scales[:],
+                lhsT=codes["w"][:, cols].bitcast(E4M3X4),
+                lhsT_scale=scales["w"][:, cols],
+                rhs=codes["dy"][:].bitcast(E5M2X4),
+                rhs_scale=scales["dy"][:],
                 start=True,
                 stop=True,
             )
-            width = max(X, *pieces[b]) + ENTRIES_PER_COLUMN
-            win = far.tile([P, width], F32, name=f"u_win{b}", offset=u_at[b])
+            win = keep.tile([P, WINDOW], F32, name=f"u_win{b}")
             nc.scalar.copy(win[:, 0:X], bank[:])
-            u_win.setdefault(b, win)
+            return win
 
-        for b in order:
-            c0 = 0
-            for n in pieces[b]:
-                entries = dst[:, c0 // ENTRIES_PER_COLUMN : (c0 + n) // ENTRIES_PER_COLUMN]
-                res = far.tile([P, n], F32, name=f"res{b}_{c0}", offset=res_at[b] + 4 * c0)
-                nc.vector.tensor_tensor(
-                    res[:], u_win[b][:].indirect(entries), xs[b][:, c0 : c0 + n], mybir.AluOpType.mult
-                )
-                nc.sync.dma_start(out[b * P : (b + 1) * P, c0 : c0 + n], res[:])
-                c0 = c0 + n
+        def store(b, c0, c1):
+            nc.sync.dma_start(out[b * P : (b + 1) * P, c0:c1], res[b][:, c0:c1])
+
+        def fused(b, c0, c1):
+            nc.vector.tensor_tensor(res[b][:, c0:c1], u_win[b][:].indirect(entries(dst, c0, c1)), xs[b][:, c0:c1], MULT)
+            store(b, c0, c1)
+
+        def look_up(b, c0, c1):
+            nc.scalar.activation(ud[b][:, c0:c1], u_win[b][:].indirect(entries(dst, c0, c1)), COPY)
+
+        def plain(b, c0, c1):
+            nc.vector.tensor_tensor(res[b][:, c0:c1], ud[b][:, c0:c1], xs[b][:, c0:c1], MULT)
+            store(b, c0, c1)
+
+        nc.vector.tensor_copy(xs[0][:], x_win[0][:].indirect(src[:]))
+        prepare(w_raw0, "w", 0, nc.scalar.copy)
+        nc.scalar.activation(xs[1][:], x_win[1][:].indirect(src[:]), COPY)
+        prepare(dy_raw0, "dy", 0)
+        nc.scalar.activation(xs[2][:], x_win[2][:].indirect(src[:]), COPY)
+        nc.vector.tensor_copy(xs[3][:, 0:X_SPLIT], x_win[3][:].indirect(entries(src, 0, X_SPLIT)))
+        nc.scalar.activation(xs[3][:, X_SPLIT:C], x_win[3][:].indirect(entries(src, X_SPLIT, C)), COPY)
+        prepare(dy_raw1, "dy", 2)
+        prepare(w_raw1, "w", 1)
+        prepare(w_raw2, "w", 2)
+
+        res = [keep.tile([P, C], F32, name=f"res{b}", tag="w2_raw" if b == 0 else f"res{b}") for b in range(4)]
+        u_win = {b: multiply(b) for b in (0, 1)}
+        fused(0, 0, C)
+        look_up(1, 0, C)
+        u_win.update({b: multiply(b) for b in (3, 2)})
+        plain(1, 0, C)
+        look_up(2, 0, 576)
+        fused(3, 0, 512)
+        plain(2, 0, 576)
+        look_up(2, 576, C)
+        fused(3, 512, 832)
+        plain(2, 576, C)
+        look_up(3, 832, C)
+        plain(3, 832, C)

@@ -20,8 +20,11 @@ PACK = 4
 PER_COLUMN = 16
 RUN = 4
 WINDOW = C + PER_COLUMN
+HALF = X // 2
+MID = C // 2
 FIRST_WINDOW = 1376
-X_SPLIT = 640
+U_SHARE = 800
+LAST_CUTS = (0, 352, 672, C)
 
 
 def tile_attend_gcfconv_f_kernel(tc, W, dyT, xT, soffs, toffs, out):
@@ -46,95 +49,105 @@ def tile_attend_gcfconv_f_kernel(tc, W, dyT, xT, soffs, toffs, out):
             nc.sync.dma_start(raw[:], mat.rearrange("(p t) c -> p t c", t=PACK)[:, :, c0:c1])
             return raw
 
-        x_win = [load_x(0, FIRST_WINDOW)]
+        x_win0 = load_x(0, FIRST_WINDOW)
         nc.sync.dma_start(src[:], soffs)
         w_raw0 = load_operand(W, 0, P, "w0")
-        x_win.append(load_x(1, WINDOW))
-        dy_raw0 = load_operand(dyT, 0, 2 * P, "dy0")
-        x_win.append(load_x(2, WINDOW))
-        x_win.append(load_x(3, WINDOW))
-        dy_raw1 = load_operand(dyT, 2 * P, X, "dy1")
+        x_win1 = load_x(1, WINDOW)
+        dy_raw0 = load_operand(dyT, 0, HALF, "dy0")
+        x_win2 = load_x(2, WINDOW)
+        dy_raw1 = load_operand(dyT, HALF, X, "dy1")
         w_raw1 = load_operand(W, P, 2 * P, "w1")
         nc.sync.dma_start(dst[:], toffs)
-        w_raw2 = load_operand(W, 2 * P, D, "w2")
+        w_raw23 = load_operand(W, 2 * P, D, "w23")
+        x_win3 = load_x(3, WINDOW)
 
-        xs = [keep.tile([P, C], F32, name=f"xs{b}") for b in range(4)]
-        ud = [keep.tile([P, C], F32, name=f"ud{b}") for b in range(4)]
-        codes = {n: keep.tile([P, X], U32, name=n + "_codes", align_bytes=64) for n in ("dy", "w")}
-        scales = {n: keep.tile([P, X], U8, name=n + "_scales", align_bytes=64) for n in ("dy", "w")}
-        fmt = {"dy": E5M2X4, "w": E4M3X4}
+        dy_codes = keep.tile([P, X], U32, name="dy_codes", align_bytes=64)
+        dy_scales = keep.tile([P, X], U8, name="dy_scales", align_bytes=64)
+        u_win = [keep.tile([P, WINDOW], F32, name=f"u_win{b}") for b in range(4)]
 
-        def prepare(raw, name, first, cast=nc.vector.tensor_copy):
-            blocks = raw[:].shape[2] // P
-            grouped = [
-                keep.tile([P, P, PACK], BF16, name=f"{name}_grouped{first + j}", align_bytes=64)
-                for j in range(blocks)
-            ]
-            for j in range(blocks):
-                cast(
-                    grouped[j][:].rearrange("p (c i) t -> p c t i", i=RUN),
-                    raw[:, :, j * P : (j + 1) * P].rearrange("p t (c i) -> p c t i", i=RUN),
-                )
-            for j in range(blocks):
-                cols = slice((first + j) * P, (first + j + 1) * P)
-                nc.vector.quantize_mx(
-                    out=codes[name][:, cols].bitcast(fmt[name]),
-                    scales=scales[name][:, cols],
-                    in_=grouped[j][:].rearrange("p c t -> p (c t)"),
-                )
+        def cast(copy, raw, j, name):
+            grouped = keep.tile([P, P, PACK], BF16, name=name + "_grouped", align_bytes=64)
+            copy(
+                grouped[:].rearrange("p (c i) t -> p c t i", i=RUN),
+                raw[:, :, j * P : (j + 1) * P].rearrange("p t (c i) -> p c t i", i=RUN),
+            )
+            return grouped[:].rearrange("p c t -> p (c t)")
 
-        def multiply(b):
-            cols = slice(b * P, (b + 1) * P)
-            bank = psum.tile([P, X], F32, name=f"bank{b}")
+        def quantise_w(grouped, b):
+            codes = keep.tile([P, P], U32, name=f"w_codes{b}", align_bytes=64)
+            scales = keep.tile([P, P], U8, name=f"w_scales{b}", align_bytes=64)
+            nc.vector.quantize_mx(out=codes[:].bitcast(E4M3X4), scales=scales[:], in_=grouped)
+            return codes, scales
+
+        def prepare_dy(raw, h):
+            grouped = [cast(nc.vector.tensor_copy, raw, j, f"dy{h}{j}") for j in range(2)]
+            for j in range(2):
+                cols = slice(h * HALF + j * P, h * HALF + (j + 1) * P)
+                nc.vector.quantize_mx(out=dy_codes[:, cols].bitcast(E5M2X4), scales=dy_scales[:, cols], in_=grouped[j])
+
+        def multiply(w, x0, x1, name):
+            bank = psum.tile([P, x1 - x0], F32, name=name)
             nc.tensor.matmul_mx(
                 out=bank[:],
-                lhsT=codes["w"][:, cols].bitcast(E4M3X4),
-                lhsT_scale=scales["w"][:, cols],
-                rhs=codes["dy"][:].bitcast(E5M2X4),
-                rhs_scale=scales["dy"][:],
+                lhsT=w[0][:].bitcast(E4M3X4),
+                lhsT_scale=w[1][:],
+                rhs=dy_codes[:, x0:x1].bitcast(E5M2X4),
+                rhs_scale=dy_scales[:, x0:x1],
                 start=True,
                 stop=True,
             )
-            win = keep.tile([P, WINDOW], F32, name=f"u_win{b}")
-            nc.scalar.copy(win[:, 0:X], bank[:])
-            return win
+            return bank
+
+        def make_u(b, w, x0, x1, copy):
+            copy(u_win[b][:, x0:x1], multiply(w, x0, x1, f"bank{b}_{x0}")[:])
+
+        def scalar_look_up(got, win, offsets, c0, c1):
+            nc.scalar.activation(got[:, c0:c1], win[:].indirect(entries(offsets, c0, c1)), COPY)
+
+        def plain(b, c0, c1, ud, xs):
+            nc.vector.tensor_tensor(res[b][:, c0:c1], ud[:, c0:c1], xs[:, c0:c1], MULT)
+
+        def fused(b, c0, c1, xs):
+            nc.vector.tensor_tensor(res[b][:, c0:c1], u_win[b][:].indirect(entries(dst, c0, c1)), xs[:, c0:c1], MULT)
 
         def store(b, c0, c1):
             nc.sync.dma_start(out[b * P : (b + 1) * P, c0:c1], res[b][:, c0:c1])
 
-        def fused(b, c0, c1):
-            nc.vector.tensor_tensor(res[b][:, c0:c1], u_win[b][:].indirect(entries(dst, c0, c1)), xs[b][:, c0:c1], MULT)
-            store(b, c0, c1)
+        xs0, xs1, xs2, ud2 = [keep.tile([P, C], F32, name=n) for n in ("xs0", "xs1", "xs2", "ud2")]
+        nc.vector.tensor_copy(xs0[:], x_win0[:].indirect(src[:]))
+        w0 = quantise_w(cast(nc.scalar.copy, w_raw0, 0, "w0"), 0)
+        scalar_look_up(xs1, x_win1, src, 0, C)
+        prepare_dy(dy_raw0, 0)
+        scalar_look_up(xs2, x_win2, src, 0, C)
+        prepare_dy(dy_raw1, 1)
+        make_u(0, w0, 0, X, nc.scalar.copy)
+        w1 = quantise_w(cast(nc.vector.tensor_copy, w_raw1, 0, "w1"), 1)
+        make_u(1, w1, 0, X, nc.scalar.copy)
+        grouped = [cast(nc.vector.tensor_copy, w_raw23, j, f"w{2 + j}") for j in range(2)]
+        w2, w3 = [quantise_w(grouped[j], 2 + j) for j in range(2)]
 
-        def look_up(b, c0, c1):
-            nc.scalar.activation(ud[b][:, c0:c1], u_win[b][:].indirect(entries(dst, c0, c1)), COPY)
-
-        def plain(b, c0, c1):
-            nc.vector.tensor_tensor(res[b][:, c0:c1], ud[b][:, c0:c1], xs[b][:, c0:c1], MULT)
-            store(b, c0, c1)
-
-        nc.vector.tensor_copy(xs[0][:], x_win[0][:].indirect(src[:]))
-        prepare(w_raw0, "w", 0, nc.scalar.copy)
-        nc.scalar.activation(xs[1][:], x_win[1][:].indirect(src[:]), COPY)
-        prepare(dy_raw0, "dy", 0)
-        nc.scalar.activation(xs[2][:], x_win[2][:].indirect(src[:]), COPY)
-        nc.vector.tensor_copy(xs[3][:, 0:X_SPLIT], x_win[3][:].indirect(entries(src, 0, X_SPLIT)))
-        nc.scalar.activation(xs[3][:, X_SPLIT:C], x_win[3][:].indirect(entries(src, X_SPLIT, C)), COPY)
-        prepare(dy_raw1, "dy", 2)
-        prepare(w_raw1, "w", 1)
-        prepare(w_raw2, "w", 2)
-
-        res = [keep.tile([P, C], F32, name=f"res{b}", tag="w2_raw" if b == 0 else f"res{b}") for b in range(4)]
-        u_win = {b: multiply(b) for b in (0, 1)}
-        fused(0, 0, C)
-        look_up(1, 0, C)
-        u_win.update({b: multiply(b) for b in (3, 2)})
-        plain(1, 0, C)
-        look_up(2, 0, 576)
-        fused(3, 0, 512)
-        plain(2, 0, 576)
-        look_up(2, 576, C)
-        fused(3, 512, 832)
-        plain(2, 576, C)
-        look_up(3, 832, C)
-        plain(3, 832, C)
+        res = [
+            keep.tile([P, C], F32, name="res0", tag="w23_raw"),
+            keep.tile([P, C], F32, name="res1", tag="w3_grouped", align_bytes=64),
+            keep.tile([P, C], F32, name="res2"),
+            keep.tile([P, C], F32, name="res3"),
+        ]
+        fused(0, 0, C, xs0)
+        store(0, 0, C)
+        make_u(2, w2, 0, X, nc.scalar.copy)
+        bank3 = multiply(w3, 0, X, "bank3")
+        ud1 = keep.tile([P, C], F32, name="ud1", tag="w_codes3", align_bytes=64)
+        scalar_look_up(ud1, u_win[1], dst, U_SHARE, C)
+        scalar_look_up(ud2, u_win[2], dst, 0, C)
+        nc.scalar.copy(u_win[3][:, 0:X], bank3[:])
+        fused(1, 0, U_SHARE, xs1)
+        plain(1, U_SHARE, C, ud1, xs1)
+        store(1, 0, C)
+        plain(2, 0, C, ud2, xs2)
+        store(2, 0, C)
+        xs3 = keep.tile([P, C], F32, name="xs3", tag="xs1")
+        for c0, c1 in zip(LAST_CUTS, LAST_CUTS[1:]):
+            scalar_look_up(xs3, x_win3, src, c0, c1)
+            fused(3, c0, c1, xs3)
+        store(3, 0, LAST_CUTS[2])
+        store(3, LAST_CUTS[2], C)

@@ -24,6 +24,17 @@ HALF = X // 2
 MID = C // 2
 FIRST_WINDOW = 1376
 U_SHARE = 800
+STRETCH = 32 * 1024
+SLOT = 6 * 1024
+LAYOUT = (
+    (("x_win0",), ("u_win0",), ("u_win3",)),
+    (("xs0",), ("xs1", "xs3"), ("xs2",)),
+    (("w23_raw", "res0"), ("w3_grouped", "res1"), ("res2",), ("res3",)),
+    (("u_win1",), ("w0_raw",), ("dy0_raw",), ("dy1_raw",), ("w1_raw",)),
+    (("w_codes3", "ud1"), ("ud2",)),
+    (("x_win1",), ("x_win2",), ("x_win3",), ("u_win2",)),
+)
+PLACE = {name: s * STRETCH + j * SLOT for s, slots in enumerate(LAYOUT) for j, names in enumerate(slots) for name in names}
 LAST_CUTS = (0, 352, 672, C)
 
 
@@ -31,21 +42,27 @@ def tile_attend_gcfconv_f_kernel(tc, W, dyT, xT, soffs, toffs, out):
     nc = tc.nc
     with ExitStack() as ctx:
         keep = ctx.enter_context(tc.tile_pool(name="keep", bufs=1))
+        far = ctx.enter_context(tc.tile_pool(name="far", bufs=1))
         psum = ctx.enter_context(tc.psum_pool(name="psum", bufs=1))
 
         src = keep.tile([P, C // PER_COLUMN], U16, name="src")
         dst = keep.tile([P, C // PER_COLUMN], U16, name="dst")
 
+        def placed(shape, dtype, name):
+            if name not in PLACE:
+                return keep.tile(shape, dtype, name=name, align_bytes=64)
+            return far.tile(shape, dtype, name=name, offset=PLACE[name], align_bytes=STRETCH if PLACE[name] == 0 else 64)
+
         def entries(offsets, c0, c1):
             return offsets[:, c0 // PER_COLUMN : c1 // PER_COLUMN]
 
         def load_x(b, width):
-            win = keep.tile([P, width], F32, name=f"x_win{b}")
+            win = placed([P, width], F32, f"x_win{b}")
             nc.sync.dma_start(win[:, 0:X], xT[b * P : (b + 1) * P, :])
             return win
 
         def load_operand(mat, c0, c1, name):
-            raw = keep.tile([P, PACK, c1 - c0], F32, name=name + "_raw")
+            raw = placed([P, PACK, c1 - c0], F32, name + "_raw")
             nc.sync.dma_start(raw[:], mat.rearrange("(p t) c -> p t c", t=PACK)[:, :, c0:c1])
             return raw
 
@@ -63,10 +80,10 @@ def tile_attend_gcfconv_f_kernel(tc, W, dyT, xT, soffs, toffs, out):
 
         dy_codes = keep.tile([P, X], U32, name="dy_codes", align_bytes=64)
         dy_scales = keep.tile([P, X], U8, name="dy_scales", align_bytes=64)
-        u_win = [keep.tile([P, WINDOW], F32, name=f"u_win{b}") for b in range(4)]
+        u_win = [placed([P, WINDOW], F32, f"u_win{b}") for b in range(4)]
 
         def cast(copy, raw, j, name):
-            grouped = keep.tile([P, P, PACK], BF16, name=name + "_grouped", align_bytes=64)
+            grouped = placed([P, P, PACK], BF16, name + "_grouped")
             copy(
                 grouped[:].rearrange("p (c i) t -> p c t i", i=RUN),
                 raw[:, :, j * P : (j + 1) * P].rearrange("p t (c i) -> p c t i", i=RUN),
@@ -74,7 +91,7 @@ def tile_attend_gcfconv_f_kernel(tc, W, dyT, xT, soffs, toffs, out):
             return grouped[:].rearrange("p c t -> p (c t)")
 
         def quantise_w(grouped, b):
-            codes = keep.tile([P, P], U32, name=f"w_codes{b}", align_bytes=64)
+            codes = placed([P, P], U32, f"w_codes{b}")
             scales = keep.tile([P, P], U8, name=f"w_scales{b}", align_bytes=64)
             nc.vector.quantize_mx(out=codes[:].bitcast(E4M3X4), scales=scales[:], in_=grouped)
             return codes, scales
@@ -113,7 +130,7 @@ def tile_attend_gcfconv_f_kernel(tc, W, dyT, xT, soffs, toffs, out):
         def store(b, c0, c1):
             nc.sync.dma_start(out[b * P : (b + 1) * P, c0:c1], res[b][:, c0:c1])
 
-        xs0, xs1, xs2, ud2 = [keep.tile([P, C], F32, name=n) for n in ("xs0", "xs1", "xs2", "ud2")]
+        xs0, xs1, xs2, ud2 = [placed([P, C], F32, n) for n in ("xs0", "xs1", "xs2", "ud2")]
         nc.vector.tensor_copy(xs0[:], x_win0[:].indirect(src[:]))
         w0 = quantise_w(cast(nc.scalar.copy, w_raw0, 0, "w0"), 0)
         scalar_look_up(xs1, x_win1, src, 0, C)
@@ -126,17 +143,12 @@ def tile_attend_gcfconv_f_kernel(tc, W, dyT, xT, soffs, toffs, out):
         grouped = [cast(nc.vector.tensor_copy, w_raw23, j, f"w{2 + j}") for j in range(2)]
         w2, w3 = [quantise_w(grouped[j], 2 + j) for j in range(2)]
 
-        res = [
-            keep.tile([P, C], F32, name="res0", tag="w23_raw"),
-            keep.tile([P, C], F32, name="res1", tag="w3_grouped", align_bytes=64),
-            keep.tile([P, C], F32, name="res2"),
-            keep.tile([P, C], F32, name="res3"),
-        ]
+        res = [placed([P, C], F32, f"res{b}") for b in range(4)]
         fused(0, 0, C, xs0)
         store(0, 0, C)
         make_u(2, w2, 0, X, nc.scalar.copy)
         bank3 = multiply(w3, 0, X, "bank3")
-        ud1 = keep.tile([P, C], F32, name="ud1", tag="w_codes3", align_bytes=64)
+        ud1 = placed([P, C], F32, "ud1")
         scalar_look_up(ud1, u_win[1], dst, U_SHARE, C)
         scalar_look_up(ud2, u_win[2], dst, 0, C)
         nc.scalar.copy(u_win[3][:, 0:X], bank3[:])
@@ -145,7 +157,7 @@ def tile_attend_gcfconv_f_kernel(tc, W, dyT, xT, soffs, toffs, out):
         store(1, 0, C)
         plain(2, 0, C, ud2, xs2)
         store(2, 0, C)
-        xs3 = keep.tile([P, C], F32, name="xs3", tag="xs1")
+        xs3 = placed([P, C], F32, "xs3")
         for c0, c1 in zip(LAST_CUTS, LAST_CUTS[1:]):
             scalar_look_up(xs3, x_win3, src, c0, c1)
             fused(3, c0, c1, xs3)

@@ -23,7 +23,7 @@ WINDOW = C + PER_COLUMN
 HALF = X // 2
 MID = C // 2
 FIRST_WINDOW = 1376
-U_SHARE = 800
+U_SHARE = 672
 STRETCH = 32 * 1024
 SLOT = 6 * 1024
 LAYOUT = (
@@ -31,11 +31,11 @@ LAYOUT = (
     (("xs0",), ("xs1", "xs3"), ("xs2",)),
     (("w23_raw", "res0"), ("w3_grouped", "res1"), ("res2",), ("res3",)),
     (("u_win1",), ("w0_raw",), ("dy0_raw",), ("dy1_raw",), ("w1_raw",)),
-    (("w_codes3", "ud1"), ("ud2",)),
+    (("ud0",), ("ud2",)),
     (("x_win1",), ("x_win2",), ("x_win3",), ("u_win2",)),
 )
 PLACE = {name: s * STRETCH + j * SLOT for s, slots in enumerate(LAYOUT) for j, names in enumerate(slots) for name in names}
-LAST_CUTS = (0, 352, 672, C)
+LAST_CUTS = (0, 352, 704, C)
 
 
 def tile_attend_gcfconv_f_kernel(tc, W, dyT, xT, soffs, toffs, out):
@@ -74,8 +74,8 @@ def tile_attend_gcfconv_f_kernel(tc, W, dyT, xT, soffs, toffs, out):
         x_win2 = load_x(2, WINDOW)
         dy_raw1 = load_operand(dyT, HALF, X, "dy1")
         w_raw1 = load_operand(W, P, 2 * P, "w1")
-        nc.sync.dma_start(dst[:], toffs)
         w_raw23 = load_operand(W, 2 * P, D, "w23")
+        nc.sync.dma_start(dst[:], toffs)
         x_win3 = load_x(3, WINDOW)
 
         dy_codes = keep.tile([P, X], U32, name="dy_codes", align_bytes=64)
@@ -144,18 +144,18 @@ def tile_attend_gcfconv_f_kernel(tc, W, dyT, xT, soffs, toffs, out):
         w2, w3 = [quantise_w(grouped[j], 2 + j) for j in range(2)]
 
         res = [placed([P, C], F32, f"res{b}") for b in range(4)]
-        fused(0, 0, C, xs0)
+        ud0 = placed([P, C], F32, "ud0")
+        scalar_look_up(ud0, u_win[0], dst, U_SHARE, C)
+        fused(0, 0, U_SHARE, xs0)
+        plain(0, U_SHARE, C, ud0, xs0)
         store(0, 0, C)
         make_u(2, w2, 0, X, nc.scalar.copy)
-        bank3 = multiply(w3, 0, X, "bank3")
-        ud1 = placed([P, C], F32, "ud1")
-        scalar_look_up(ud1, u_win[1], dst, U_SHARE, C)
-        scalar_look_up(ud2, u_win[2], dst, 0, C)
-        nc.scalar.copy(u_win[3][:, 0:X], bank3[:])
-        fused(1, 0, U_SHARE, xs1)
-        plain(1, U_SHARE, C, ud1, xs1)
+        make_u(3, w3, 0, X, nc.scalar.copy)
+        fused(1, 0, C, xs1)
         store(1, 0, C)
-        plain(2, 0, C, ud2, xs2)
+        for c0 in (0, MID):
+            scalar_look_up(ud2, u_win[2], dst, c0, c0 + MID)
+            plain(2, c0, c0 + MID, ud2, xs2)
         store(2, 0, C)
         xs3 = placed([P, C], F32, "xs3")
         for c0, c1 in zip(LAST_CUTS, LAST_CUTS[1:]):

@@ -23,19 +23,20 @@ WINDOW = C + PER_COLUMN
 HALF = X // 2
 MID = C // 2
 FIRST_WINDOW = 1376
-U_SHARE = 672
+U_SHARE = 704
+X_SHARE = 192
 STRETCH = 32 * 1024
-SLOT = 6 * 1024
+SLOT = 8 * 1024
 LAYOUT = (
-    (("x_win0",), ("u_win0",), ("u_win3",)),
-    (("xs0",), ("xs1", "xs3"), ("xs2",)),
-    (("w23_raw", "res0"), ("w3_grouped", "res1"), ("res2",), ("res3",)),
-    (("u_win1",), ("w0_raw",), ("dy0_raw",), ("dy1_raw",), ("w1_raw",)),
-    (("ud0",), ("ud2",)),
+    (("x_win0",), ("u_win0",), ("u_win1",), ("u_win3",)),
+    (("xs0", "xs3"), ("xs1",), ("xs2",), ("w1_grouped", "ud0")),
+    (("ud2",), ("dy_codes",), ("xs3_first",), ("w1_codes",)),
+    (("w123_raw", "res0"), ("w23_codes", "res1"), ("res2",), ("res3",)),
+    (("w0_raw",), ("dy_raw",)),
     (("x_win1",), ("x_win2",), ("x_win3",), ("u_win2",)),
 )
 PLACE = {name: s * STRETCH + j * SLOT for s, slots in enumerate(LAYOUT) for j, names in enumerate(slots) for name in names}
-LAST_CUTS = (0, 352, 704, C)
+LAST_CUTS = (0, 256, 640, 896, C)
 
 
 def tile_attend_gcfconv_f_kernel(tc, W, dyT, xT, soffs, toffs, out):
@@ -70,44 +71,37 @@ def tile_attend_gcfconv_f_kernel(tc, W, dyT, xT, soffs, toffs, out):
         nc.sync.dma_start(src[:], soffs)
         w_raw0 = load_operand(W, 0, P, "w0")
         x_win1 = load_x(1, WINDOW)
-        dy_raw0 = load_operand(dyT, 0, HALF, "dy0")
+        dy_raw = load_operand(dyT, 0, X, "dy")
         x_win2 = load_x(2, WINDOW)
-        dy_raw1 = load_operand(dyT, HALF, X, "dy1")
-        w_raw1 = load_operand(W, P, 2 * P, "w1")
-        w_raw23 = load_operand(W, 2 * P, D, "w23")
+        w_raw123 = load_operand(W, P, D, "w123")
         nc.sync.dma_start(dst[:], toffs)
         x_win3 = load_x(3, WINDOW)
 
-        dy_codes = keep.tile([P, X], U32, name="dy_codes", align_bytes=64)
+        dy_codes = placed([P, X], U32, "dy_codes")
         dy_scales = keep.tile([P, X], U8, name="dy_scales", align_bytes=64)
         u_win = [placed([P, WINDOW], F32, f"u_win{b}") for b in range(4)]
 
-        def cast(copy, raw, j, name):
-            grouped = placed([P, P, PACK], BF16, name + "_grouped")
+        def cast(copy, raw, c0, c1, name):
+            grouped = placed([P, c1 - c0, PACK], BF16, name + "_grouped")
             copy(
                 grouped[:].rearrange("p (c i) t -> p c t i", i=RUN),
-                raw[:, :, j * P : (j + 1) * P].rearrange("p t (c i) -> p c t i", i=RUN),
+                raw[:, :, c0:c1].rearrange("p t (c i) -> p c t i", i=RUN),
             )
             return grouped[:].rearrange("p c t -> p (c t)")
 
-        def quantise_w(grouped, b):
-            codes = placed([P, P], U32, f"w_codes{b}")
-            scales = keep.tile([P, P], U8, name=f"w_scales{b}", align_bytes=64)
+        def quantise_w(grouped, name):
+            width = grouped.shape[1] // PACK
+            codes = placed([P, width], U32, name + "_codes")
+            scales = placed([P, width], U8, name + "_scales")
             nc.vector.quantize_mx(out=codes[:].bitcast(E4M3X4), scales=scales[:], in_=grouped)
-            return codes, scales
-
-        def prepare_dy(raw, h):
-            grouped = [cast(nc.vector.tensor_copy, raw, j, f"dy{h}{j}") for j in range(2)]
-            for j in range(2):
-                cols = slice(h * HALF + j * P, h * HALF + (j + 1) * P)
-                nc.vector.quantize_mx(out=dy_codes[:, cols].bitcast(E5M2X4), scales=dy_scales[:, cols], in_=grouped[j])
+            return [(codes[:, c0 : c0 + P], scales[:, c0 : c0 + P]) for c0 in range(0, width, P)]
 
         def multiply(w, x0, x1, name):
             bank = psum.tile([P, x1 - x0], F32, name=name)
             nc.tensor.matmul_mx(
                 out=bank[:],
-                lhsT=w[0][:].bitcast(E4M3X4),
-                lhsT_scale=w[1][:],
+                lhsT=w[0].bitcast(E4M3X4),
+                lhsT_scale=w[1],
                 rhs=dy_codes[:, x0:x1].bitcast(E5M2X4),
                 rhs_scale=dy_scales[:, x0:x1],
                 start=True,
@@ -132,16 +126,19 @@ def tile_attend_gcfconv_f_kernel(tc, W, dyT, xT, soffs, toffs, out):
 
         xs0, xs1, xs2, ud2 = [placed([P, C], F32, n) for n in ("xs0", "xs1", "xs2", "ud2")]
         nc.vector.tensor_copy(xs0[:], x_win0[:].indirect(src[:]))
-        w0 = quantise_w(cast(nc.scalar.copy, w_raw0, 0, "w0"), 0)
+        (w0,) = quantise_w(cast(nc.scalar.copy, w_raw0, 0, P, "w0"), "w0")
         scalar_look_up(xs1, x_win1, src, 0, C)
-        prepare_dy(dy_raw0, 0)
-        scalar_look_up(xs2, x_win2, src, 0, C)
-        prepare_dy(dy_raw1, 1)
+        scalar_look_up(xs2, x_win2, src, X_SHARE, C)
+        grouped = [cast(nc.vector.tensor_copy, dy_raw, c0, c0 + HALF, f"dy{c0}") for c0 in (0, HALF)]
+        for c0, half in zip((0, HALF), grouped):
+            cols = slice(c0, c0 + HALF)
+            nc.vector.quantize_mx(out=dy_codes[:, cols].bitcast(E5M2X4), scales=dy_scales[:, cols], in_=half)
         make_u(0, w0, 0, X, nc.scalar.copy)
-        w1 = quantise_w(cast(nc.vector.tensor_copy, w_raw1, 0, "w1"), 1)
-        make_u(1, w1, 0, X, nc.scalar.copy)
-        grouped = [cast(nc.vector.tensor_copy, w_raw23, j, f"w{2 + j}") for j in range(2)]
-        w2, w3 = [quantise_w(grouped[j], 2 + j) for j in range(2)]
+        nc.vector.tensor_copy(xs2[:, 0:X_SHARE], x_win2[:].indirect(entries(src, 0, X_SHARE)))
+        grouped1 = cast(nc.vector.tensor_copy, w_raw123, 0, P, "w1")
+        grouped23 = cast(nc.vector.tensor_copy, w_raw123, P, 3 * P, "w23")
+        (w1,) = quantise_w(grouped1, "w1")
+        w2, w3 = quantise_w(grouped23, "w23")
 
         res = [placed([P, C], F32, f"res{b}") for b in range(4)]
         ud0 = placed([P, C], F32, "ud0")
@@ -149,17 +146,30 @@ def tile_attend_gcfconv_f_kernel(tc, W, dyT, xT, soffs, toffs, out):
         fused(0, 0, U_SHARE, xs0)
         plain(0, U_SHARE, C, ud0, xs0)
         store(0, 0, C)
+        make_u(1, w1, 0, X, nc.scalar.copy)
+        first = LAST_CUTS[1]
+        xs3_first = placed([P, first], F32, "xs3_first")
+        scalar_look_up(xs3_first, x_win3, src, 0, first)
         make_u(2, w2, 0, X, nc.scalar.copy)
         make_u(3, w3, 0, X, nc.scalar.copy)
         fused(1, 0, C, xs1)
         store(1, 0, C)
-        for c0 in (0, MID):
+        fused(3, 0, first, xs3_first)
+        xs3 = placed([P, C], F32, "xs3")
+
+        def plain_half(c0):
             scalar_look_up(ud2, u_win[2], dst, c0, c0 + MID)
             plain(2, c0, c0 + MID, ud2, xs2)
-        store(2, 0, C)
-        xs3 = placed([P, C], F32, "xs3")
-        for c0, c1 in zip(LAST_CUTS, LAST_CUTS[1:]):
+            store(2, c0, c0 + MID)
+
+        def fused_piece(j, stored_from):
+            c0, c1 = LAST_CUTS[j : j + 2]
             scalar_look_up(xs3, x_win3, src, c0, c1)
             fused(3, c0, c1, xs3)
-        store(3, 0, LAST_CUTS[2])
-        store(3, LAST_CUTS[2], C)
+            store(3, stored_from, c1)
+
+        plain_half(0)
+        fused_piece(1, 0)
+        plain_half(MID)
+        fused_piece(2, LAST_CUTS[2])
+        fused_piece(3, LAST_CUTS[3])

@@ -57,9 +57,9 @@ def tile_attend_gcfconv_f_kernel(tc, W, dyT, xT, soffs, toffs, out):
         def entries(offsets, c0, c1):
             return offsets[:, c0 // PER_COLUMN : c1 // PER_COLUMN]
 
-        def load_x(b, width):
+        def load_x(b, width, queue):
             win = placed([P, width], F32, f"x_win{b}")
-            nc.sync.dma_start(win[:, 0:X], xT[b * P : (b + 1) * P, :])
+            queue.dma_start(win[:, 0:X], xT[b * P : (b + 1) * P, :])
             return win
 
         def load_operand(mat, c0, c1, name):
@@ -67,15 +67,15 @@ def tile_attend_gcfconv_f_kernel(tc, W, dyT, xT, soffs, toffs, out):
             nc.sync.dma_start(raw[:], mat.rearrange("(p t) c -> p t c", t=PACK)[:, :, c0:c1])
             return raw
 
-        x_win0 = load_x(0, FIRST_WINDOW)
+        x_win0 = load_x(0, FIRST_WINDOW, nc.scalar)
         nc.sync.dma_start(src[:], soffs)
         w_raw0 = load_operand(W, 0, P, "w0")
-        x_win1 = load_x(1, WINDOW)
+        x_win1 = load_x(1, WINDOW, nc.scalar)
         dy_raw = load_operand(dyT, 0, X, "dy")
-        x_win2 = load_x(2, WINDOW)
+        x_win2 = load_x(2, WINDOW, nc.sync)
         w_raw123 = load_operand(W, P, D, "w123")
+        x_win3 = load_x(3, WINDOW, nc.sync)
         nc.sync.dma_start(dst[:], toffs)
-        x_win3 = load_x(3, WINDOW)
 
         dy_codes = placed([P, X], U32, "dy_codes")
         dy_scales = keep.tile([P, X], U8, name="dy_scales", align_bytes=64)

@@ -36,7 +36,7 @@ LAYOUT = (
     (("x_win1",), ("x_win2",), ("x_win3",), ("u_win2",)),
 )
 PLACE = {name: s * STRETCH + j * SLOT for s, slots in enumerate(LAYOUT) for j, names in enumerate(slots) for name in names}
-LAST_CUTS = (0, 256, 640, 896, C)
+LAST_CUTS = (0, 256, 576, 832, C)
 
 
 def tile_attend_gcfconv_f_kernel(tc, W, dyT, xT, soffs, toffs, out):

@@ -124,6 +124,10 @@ def tile_attend_gcfconv_f_kernel(tc, W, dyT, xT, soffs, toffs, out):
         def store(b, c0, c1):
             nc.sync.dma_start(out[b * P : (b + 1) * P, c0:c1], res[b][:, c0:c1])
 
+        def store_quarters(b, c0, c1):
+            for q0 in range(c0, c1, C // 4):
+                store(b, q0, q0 + C // 4)
+
         xs0, xs1, xs2, ud2 = [placed([P, C], F32, n) for n in ("xs0", "xs1", "xs2", "ud2")]
         nc.vector.tensor_copy(xs0[:], x_win0[:].indirect(src[:]))
         (w0,) = quantise_w(cast(nc.scalar.copy, w_raw0, 0, P, "w0"), "w0")
@@ -144,32 +148,35 @@ def tile_attend_gcfconv_f_kernel(tc, W, dyT, xT, soffs, toffs, out):
         ud0 = placed([P, C], F32, "ud0")
         scalar_look_up(ud0, u_win[0], dst, U_SHARE, C)
         fused(0, 0, U_SHARE, xs0)
+        store_quarters(0, 0, MID)
         plain(0, U_SHARE, C, ud0, xs0)
-        store(0, 0, C)
+        store_quarters(0, MID, C)
         make_u(1, w1, 0, X, nc.scalar.copy)
         first = LAST_CUTS[1]
         xs3_first = placed([P, first], F32, "xs3_first")
         scalar_look_up(xs3_first, x_win3, src, 0, first)
         make_u(2, w2, 0, X, nc.scalar.copy)
         make_u(3, w3, 0, X, nc.scalar.copy)
-        fused(1, 0, C, xs1)
-        store(1, 0, C)
+        for c0 in (0, MID):
+            fused(1, c0, c0 + MID, xs1)
+            store_quarters(1, c0, c0 + MID)
         fused(3, 0, first, xs3_first)
+        store(3, 0, first)
         xs3 = placed([P, C], F32, "xs3")
 
-        def plain_half(c0):
+        def plain_half(c0, stored):
             scalar_look_up(ud2, u_win[2], dst, c0, c0 + MID)
             plain(2, c0, c0 + MID, ud2, xs2)
-            store(2, c0, c0 + MID)
+            stored(2, c0, c0 + MID)
 
-        def fused_piece(j, stored_from):
+        def fused_piece(j):
             c0, c1 = LAST_CUTS[j : j + 2]
             scalar_look_up(xs3, x_win3, src, c0, c1)
             fused(3, c0, c1, xs3)
-            store(3, stored_from, c1)
+            store(3, c0, c1)
 
-        plain_half(0)
-        fused_piece(1, 0)
-        plain_half(MID)
-        fused_piece(2, LAST_CUTS[2])
-        fused_piece(3, LAST_CUTS[3])
+        plain_half(0, store_quarters)
+        fused_piece(1)
+        plain_half(MID, store)
+        fused_piece(2)
+        fused_piece(3)

@@ -23,7 +23,7 @@ WINDOW = C + PER_COLUMN
 HALF = X // 2
 MID = C // 2
 FIRST_WINDOW = 1376
-U_SHARE = 704
+U_SHARE = 640
 X_SHARE = 192
 STRETCH = 32 * 1024
 SLOT = 8 * 1024
@@ -36,7 +36,7 @@ LAYOUT = (
     (("x_win1",), ("x_win2",), ("x_win3",), ("u_win2",)),
 )
 PLACE = {name: s * STRETCH + j * SLOT for s, slots in enumerate(LAYOUT) for j, names in enumerate(slots) for name in names}
-LAST_CUTS = (0, 256, 576, 832, C)
+LAST_CUTS = (0, 192, 576, 832, C)
 
 
 def tile_attend_gcfconv_f_kernel(tc, W, dyT, xT, soffs, toffs, out):

from contextlib import ExitStack

import concourse.mybir as mybir

M, D, X, C = 512, 512, 512, 1024
FLOPS = 2 * M * D * X

F32 = mybir.dt.float32
BF16 = mybir.dt.bfloat16
U32 = mybir.dt.uint32
U16 = mybir.dt.uint16
U8 = mybir.dt.uint8
E4M3X4 = mybir.dt.float8_e4m3fn_x4
E5M2X4 = mybir.dt.float8_e5m2_x4
COPY = mybir.ActivationFunctionType.Copy
MULT = mybir.AluOpType.mult

P = 128
PACK = 4
PER_COLUMN = 16
RUN = 4
WINDOW = C + PER_COLUMN
HALF = X // 2
MID = C // 2
FIRST_WINDOW = 1376
U_SHARE = 640
X_SHARE = 192
STRETCH = 32 * 1024
SLOT = 8 * 1024
LAYOUT = (
    (("x_win0",), ("u_win0",), ("u_win1",), ("u_win3",)),
    (("xs0", "xs3"), ("xs1",), ("xs2",), ("w1_grouped", "ud0")),
    (("ud2",), ("dy_codes",), ("xs3_first",), ("w1_codes",)),
    (("w123_raw", "res0"), ("w23_codes", "res1"), ("res2",), ("res3",)),
    (("w0_raw",), ("dy_raw",)),
    (("x_win1",), ("x_win2",), ("x_win3",), ("u_win2",)),
)
PLACE = {name: s * STRETCH + j * SLOT for s, slots in enumerate(LAYOUT) for j, names in enumerate(slots) for name in names}
LAST_CUTS = (0, 192, 576, 832, C)


def tile_attend_gcfconv_f_kernel(tc, W, dyT, xT, soffs, toffs, out):
    nc = tc.nc
    with ExitStack() as ctx:
        keep = ctx.enter_context(tc.tile_pool(name="keep", bufs=1))
        far = ctx.enter_context(tc.tile_pool(name="far", bufs=1))
        psum = ctx.enter_context(tc.psum_pool(name="psum", bufs=1))

        src = keep.tile([P, C // PER_COLUMN], U16, name="src")
        dst = keep.tile([P, C // PER_COLUMN], U16, name="dst")

        def placed(shape, dtype, name):
            if name not in PLACE:
                return keep.tile(shape, dtype, name=name, align_bytes=64)
            return far.tile(shape, dtype, name=name, offset=PLACE[name], align_bytes=STRETCH if PLACE[name] == 0 else 64)

        def entries(offsets, c0, c1):
            return offsets[:, c0 // PER_COLUMN : c1 // PER_COLUMN]

        def load_x(b, width, queue):
            win = placed([P, width], F32, f"x_win{b}")
            queue.dma_start(win[:, 0:X], xT[b * P : (b + 1) * P, :])
            return win

        def load_operand(mat, c0, c1, name):
            raw = placed([P, PACK, c1 - c0], F32, name + "_raw")
            nc.sync.dma_start(raw[:], mat.rearrange("(p t) c -> p t c", t=PACK)[:, :, c0:c1])
            return raw

        x_win0 = load_x(0, FIRST_WINDOW, nc.scalar)
        nc.sync.dma_start(src[:], soffs)
        w_raw0 = load_operand(W, 0, P, "w0")
        x_win1 = load_x(1, WINDOW, nc.scalar)
        dy_raw = load_operand(dyT, 0, X, "dy")
        x_win2 = load_x(2, WINDOW, nc.sync)
        w_raw123 = load_operand(W, P, D, "w123")
        x_win3 = load_x(3, WINDOW, nc.sync)
        nc.sync.dma_start(dst[:], toffs)

        dy_codes = placed([P, X], U32, "dy_codes")
        dy_scales = keep.tile([P, X], U8, name="dy_scales", align_bytes=64)
        u_win = [placed([P, WINDOW], F32, f"u_win{b}") for b in range(4)]

        def cast(copy, raw, c0, c1, name):
            grouped = placed([P, c1 - c0, PACK], BF16, name + "_grouped")
            copy(
                grouped[:].rearrange("p (c i) t -> p c t i", i=RUN),
                raw[:, :, c0:c1].rearrange("p t (c i) -> p c t i", i=RUN),
            )
            return grouped[:].rearrange("p c t -> p (c t)")

        def quantise_w(grouped, name):
            width = grouped.shape[1] // PACK
            codes = placed([P, width], U32, name + "_codes")
            scales = placed([P, width], U8, name + "_scales")
            nc.vector.quantize_mx(out=codes[:].bitcast(E4M3X4), scales=scales[:], in_=grouped)
            return [(codes[:, c0 : c0 + P], scales[:, c0 : c0 + P]) for c0 in range(0, width, P)]

        def multiply(w, x0, x1, name):
            bank = psum.tile([P, x1 - x0], F32, name=name)
            nc.tensor.matmul_mx(
                out=bank[:],
                lhsT=w[0].bitcast(E4M3X4),
                lhsT_scale=w[1],
                rhs=dy_codes[:, x0:x1].bitcast(E5M2X4),
                rhs_scale=dy_scales[:, x0:x1],
                start=True,
                stop=True,
            )
            return bank

        def make_u(b, w, x0, x1, copy):
            copy(u_win[b][:, x0:x1], multiply(w, x0, x1, f"bank{b}_{x0}")[:])

        def scalar_look_up(got, win, offsets, c0, c1):
            nc.scalar.activation(got[:, c0:c1], win[:].indirect(entries(offsets, c0, c1)), COPY)

        def plain(b, c0, c1, ud, xs):
            nc.vector.tensor_tensor(res[b][:, c0:c1], ud[:, c0:c1], xs[:, c0:c1], MULT)

        def fused(b, c0, c1, xs):
            nc.vector.tensor_tensor(res[b][:, c0:c1], u_win[b][:].indirect(entries(dst, c0, c1)), xs[:, c0:c1], MULT)

        def store(b, c0, c1):
            nc.sync.dma_start(out[b * P : (b + 1) * P, c0:c1], res[b][:, c0:c1])

        def store_quarters(b, c0, c1):
            for q0 in range(c0, c1, C // 4):
                store(b, q0, q0 + C // 4)

        xs0, xs1, xs2, ud2 = [placed([P, C], F32, n) for n in ("xs0", "xs1", "xs2", "ud2")]
        nc.vector.tensor_copy(xs0[:], x_win0[:].indirect(src[:]))
        (w0,) = quantise_w(cast(nc.scalar.copy, w_raw0, 0, P, "w0"), "w0")
        scalar_look_up(xs1, x_win1, src, 0, C)
        scalar_look_up(xs2, x_win2, src, X_SHARE, C)
        grouped = [cast(nc.vector.tensor_copy, dy_raw, c0, c0 + HALF, f"dy{c0}") for c0 in (0, HALF)]
        for c0, half in zip((0, HALF), grouped):
            cols = slice(c0, c0 + HALF)
            nc.vector.quantize_mx(out=dy_codes[:, cols].bitcast(E5M2X4), scales=dy_scales[:, cols], in_=half)
        make_u(0, w0, 0, X, nc.scalar.copy)
        nc.vector.tensor_copy(xs2[:, 0:X_SHARE], x_win2[:].indirect(entries(src, 0, X_SHARE)))
        grouped1 = cast(nc.vector.tensor_copy, w_raw123, 0, P, "w1")
        grouped23 = cast(nc.vector.tensor_copy, w_raw123, P, 3 * P, "w23")
        (w1,) = quantise_w(grouped1, "w1")
        w2, w3 = quantise_w(grouped23, "w23")

        res = [placed([P, C], F32, f"res{b}") for b in range(4)]
        ud0 = placed([P, C], F32, "ud0")
        scalar_look_up(ud0, u_win[0], dst, U_SHARE, C)
        fused(0, 0, U_SHARE, xs0)
        store_quarters(0, 0, MID)
        plain(0, U_SHARE, C, ud0, xs0)
        store_quarters(0, MID, C)
        make_u(1, w1, 0, X, nc.scalar.copy)
        first = LAST_CUTS[1]
        xs3_first = placed([P, first], F32, "xs3_first")
        scalar_look_up(xs3_first, x_win3, src, 0, first)
        make_u(2, w2, 0, X, nc.scalar.copy)
        make_u(3, w3, 0, X, nc.scalar.copy)
        for c0 in (0, MID):
            fused(1, c0, c0 + MID, xs1)
            store_quarters(1, c0, c0 + MID)
        fused(3, 0, first, xs3_first)
        store(3, 0, first)
        xs3 = placed([P, C], F32, "xs3")

        def plain_half(c0, stored):
            scalar_look_up(ud2, u_win[2], dst, c0, c0 + MID)
            plain(2, c0, c0 + MID, ud2, xs2)
            stored(2, c0, c0 + MID)

        def fused_piece(j):
            c0, c1 = LAST_CUTS[j : j + 2]
            scalar_look_up(xs3, x_win3, src, c0, c1)
            fused(3, c0, c1, xs3)
            store(3, c0, c1)

        plain_half(0, store_quarters)
        fused_piece(1)
        plain_half(MID, store)
        fused_piece(2)
        fused_piece(3)
